import numpy as np, ml_dtypes
CORES = [24,25,26,27,28,29,30,31]
N = 8
import mx_ref
BF = ml_dtypes.bfloat16
def gcols(t, e):
    v = np.concatenate([t.reshape(8, 16, -1, 4), np.zeros((8, 16, 1, 4), BF)], axis=2)
    return np.ascontiguousarray(np.stack([v[g][:, e[g]] for g in range(8)])).reshape(128, -1)
def tile(rs):
    return np.stack(rs, axis=2).reshape(128, -1).astype(BF)
def pick(q, e):
    c = np.concatenate([q[0].reshape(128, -1, 4), np.zeros((128, 1, 4), np.uint8)], axis=1); s = np.concatenate([q[1], np.ones((16, 1), np.uint8)], axis=1)
    return (np.ascontiguousarray(c[:, e].reshape(128, -1)), np.ascontiguousarray(s[:, e]))
def join(*qs):
    return (np.concatenate([q[0] for q in qs], axis=1), np.concatenate([q[1] for q in qs], axis=1))
def put(q, e, v):
    c, s = q[0].reshape(128, -1, 4).copy(), q[1].copy(); c[:, e] = v[0].reshape(128, -1, 4); s[:, e] = v[1]
    return (c.reshape(128, -1), s)
def pk(c, s):
    return (np.ascontiguousarray(c), mx_ref.live(s))
def emit(q):
    return q[0], q[1]
def packed(v, rng):
    q = [mx_ref.quantize(np.ascontiguousarray(v[r])) for r in range(N)]
    return np.stack([a for a, b in q]), np.stack([mx_ref.plane(b, rng) for a, b in q])
def values_of_codes():
    e, c = np.zeros((128, 128, 4), np.float32), np.zeros((128, 2, 4), np.uint8)
    e[np.arange(128), np.arange(128), 0] = 1
    c[:127, :, 0] = np.arange(256).reshape(2, 128).T[:127]
    return mx_ref.matmul(mx_ref.quantize(e.reshape(128, 512).astype(BF)), (c.reshape(128, 8), np.full((16, 2), 127, np.uint8))).T.reshape(-1).astype(np.float64)
CODE_VALUE, SCALE_VALUE = values_of_codes(), 2.0 ** (np.arange(256) - 127.0)
def decode(q):
    return (CODE_VALUE[q[0]].reshape(16, 8, -1, 4) * SCALE_VALUE[q[1]][:, None, :, None] + 0.0).reshape(128, -1).astype(np.float32)
def f(rng, *shape):
    return mx_ref.flush((rng.standard_normal(shape, dtype=np.float32) * np.exp2(rng.integers(-2, 3, shape[:-1] + (1,)))).astype(BF))
def wide(rng, *shape, cols=0):
    v = rng.standard_normal(shape, dtype=np.float32) * np.exp2(rng.integers(-12, 13, shape)).astype(np.float32)
    if cols: v *= np.repeat(np.exp2(rng.integers(-cols, cols + 1, shape[:-2] + (1, shape[-1] // 4))) * (rng.random(shape[:-2] + (1, shape[-1] // 4)) > 0.0625), 4, axis=-1).astype(np.float32)
    return mx_ref.flush(v.astype(BF))
C, H, B, P, R = 256, 128, 64, 3, 3
def addresses(s, c):
    key = np.sum((s > 0).reshape(8, 16, -1) * (1 << np.arange(16))[:, None], axis=1)
    return B * np.arange(3)[:, None] + ((key[:, None] * c.astype(np.int64)[:, None] >> 8) & (B - 1))
def written(d, a):
    left, peel, own = np.ones((8, H), bool), np.full((8, H), -1), np.zeros((8, H), int)
    for p in range(P):
        alone = np.zeros((8, 3, H), bool)
        for g in range(8): alone[g] = np.bincount(a[g][:, left[g]].reshape(-1), minlength=3 * B)[a[g]] == 1
        taken = left & alone.any(axis=1)
        peel[taken] = p
        own[taken] = np.argmax(alone, axis=1)[taken]
        left = left & ~taken
    cell, one, two = [np.take_along_axis(a, k[:, None], axis=1)[:, 0] for k in (own, np.where(own == 0, 1, 0), np.where(own == 2, 1, 2))]
    z = np.zeros((128, 12 * B), BF)
    for p in range(P - 1, -1, -1):
        n = ((d.astype(np.float32) - gcols(z, one).astype(np.float32)) - gcols(z, two).astype(np.float32)).astype(BF).reshape(8, 16, H, 4)
        w = z.reshape(8, 16, 3 * B, 4)
        for g in range(8): w[g][:, cell[g, peel[g] == p]] = n[g][:, peel[g] == p]
    return z
def big(v):
    v = v.astype(np.float32)
    v[np.abs(v) < np.float32(2.0 ** -16)] = 0
    return v.astype(BF)
def same(v):
    return np.repeat(v[None], N, axis=0)
def numbers_of(rng):
    return {"x": big(f(rng, N, 128, 4 * C)), "u": same(np.array(f(rng, 128, 512))), "v": np.array(f(rng, N, 128, 512))}
def weights(rng, still=0):
    w = big(f(rng, N, 128, 2048)).reshape(N, 8, 16, 4, 8, 16, 4)
    w[:, :, :, :, :, :still] = 0
    c, p = packed(w.reshape(N, 128, 2048), rng)
    return {"wc": c, "ws": p}
def factors(c):
    return {"hc": np.zeros((N, 128, 3), np.int32) + np.asarray(c).astype(np.int32)}
def odd(rng):
    return rng.permutation(128)[:3] * 2 + 1
def three(a, b):
    c = -a - b
    return np.array([[a, b, c], [b, c, a]]).reshape(2, -1)
def marked(rng, keys, size, k, fine=False):
    d = numbers_of(rng)
    x = d["x"].reshape(N, 8, 16, C, 4)
    x[:, :, :8] = 0
    u = np.zeros((128, 128, 4), np.float32)
    for i in range(16):
        m = np.where((keys >> i) & 1 == 1, 1, -rng.integers(0, 2, keys.shape)) * size
        x[:, :, i // 4, :, i % 4] = (m * np.where(fine, -1.25, 1.0) + 0.0).astype(np.float32).astype(BF)
        x[:, :, 4 + i // 4, :, i % 4] = (m * np.where(fine, 1.125, 0.0) + 0.0).astype(np.float32).astype(BF)
        for h in range(0, 128, 16):
            u[h + i // 4, h + i, i % 4] = k
            u[h + 4 + i // 4, h + i, i % 4] = 1.125 * k
    return {"x": x.reshape(N, 128, 4 * C), "u": same(u.reshape(128, 512).astype(BF)), "v": d["v"], **weights(rng, 8)}
def setup_inputs(rng):
    return {**numbers_of(rng), **weights(rng), **factors(odd(rng))}
def setup_inputs_near(rng):
    size = np.where(rng.permutation(N) < N // 2, 2.0 ** -30, 1.0)
    return {**marked(rng, rng.integers(0, 65536, (N, 8, C)), size[:, None, None], 2.0 ** -30), **factors(odd(rng))}
def setup_inputs_loads(rng):
    keys = rng.integers(0, 65536, (N, 8, C))
    size, fine = np.ones((N, 8, C)), np.zeros((N, 8, C), bool)
    n, last, j, cell = np.arange(H), np.full(H, B - 1), np.arange(28), np.arange(64)
    y = cell[cell % 8 > 0]
    q = y[y < 57]
    own = np.concatenate([[cell[8:], -cell[8:] & 56], [-y & 7, y], [q & 7, q & 56]], axis=1)
    second = np.concatenate([three(9 + 2 * j[:14], 37 + 2 * j[:14]), three(j // 4 * 8, j % 4 * 2 + 1), [[8, 4], [0, 4]]], axis=1)
    deep = np.concatenate([three(6 - 4 * j[:6], -18 - 4 * j[:6]), three(17 + 2 * j[:12], 41 + 2 * j[:12]), three(j[:24] // 4 * 8, j[:24] % 4 * 2 + 1)], axis=1)
    chains = [np.pad(k, ((0, 0), (0, H - k.shape[1]))) for k in (second, deep)]
    sign = np.concatenate([np.tile([1, 1, 1, -1, -1, -1], 3), np.tile([1, 1, 1, 0, 0, 0, 0, 0, 0, -1, -1, -1], 3), np.zeros(H - 54, int)])
    large = (6 - 4 * np.array([0, 1, 2, 9, 10, 11])) & 63
    asks = np.array([(s[i], s[k]) for s in ((6, -34, 28), (2, -30, 28), (2, -38, 36), (-2, -34, 36)) for i in range(3) for k in range(3) if i != k]).T
    first = [rng.permutation(8) for r in range(N)]
    shift = rng.integers(0, 64, (N, 2, 2, 2, 1))
    spot = []
    for r in range(N):
        for h in range(2):
            lo = H * h
            m = np.where(n < 128, n, rng.integers(10, 51, H))
            l = m.copy()
            l[0] = rng.integers(10, 51)
            s = last.copy()
            s[0] = 5
            o = first[r]
            if h == 1:
                e = first[r - 1][[2, 5, 6]]
                o = np.zeros(8, int)
                o[[3, 4, 7]] = e
                o[[0, 1, 2, 5, 6]] = rng.permutation(np.setdiff1d(np.arange(8), e))
            most = own[:, rng.permutation(161)[:H]]
            for i, (a, b) in enumerate([(last, last), (s, last), most, ((m + 1) // 2, m // 2), ((l + 1) // 2, l // 2)] + [chains[k] + shift[r, h, k] for k in range(2)]):
                e = rng.permutation(H)
                keys[r, o[i], lo + e] = ((a & 63) << 8) + ((b & 63) << 2) + (rng.integers(0, 4, H) << 14)
            fine[r, o[2], lo:lo + H] = True
            size[r, o[2], lo:lo + H] = 2.0 ** -30
            if h == 0: spot.append(e)
            if h == 1:
                k = keys[r, o[7], H:].copy()
                p, t = shift[r - 1, 0, 1]
                hit = np.isin(((k >> 8) - p) & 63, large) | np.isin(((k >> 2) - t) & 63, large) | np.isin((p + t - (k * 65 >> 8)) & 63, large)
                hit[rng.permutation(H)[:24]] = True
                i = np.flatnonzero(hit)
                a, b = asks[:, np.arange(len(i)) % 24]
                keys[r, o[7], H + i] = (((a + p) & 63) << 8) + (((b + t) & 63) << 2) + (rng.integers(0, 4, len(i)) << 14)
    d = marked(rng, keys, size, 2.0 ** -30, fine)
    x = d["x"].reshape(N, 8, 16, C, 4)
    i = np.flatnonzero(sign)
    for r in range(N):
        v = rng.choice([-1.0, 1.0], (8, 1, 4)) * 2.0 ** 28
        x[r, first[r][6], 8:][:, spot[r][i]] = (v * sign[i][:, None]).astype(np.float32).astype(BF)
    return {"x": x.reshape(N, 128, 4 * C), "u": d["u"], "v": d["v"], "wc": d["wc"], "ws": d["ws"], **factors(rng.permutation([1, 64, 65]))}
def setup_inputs_huge(rng):
    d = numbers_of(rng)
    x = rng.choice([-1.0, 1.0], (N, 128, C, 4)) * (0.6 + 0.2 * rng.random((N, 128, C, 4))) * 2.0 ** 24
    u = rng.choice([-1.0, 1.0], (128, 128, 4)) * (0.75 + 0.25 * rng.random((128, 128, 4))) * 2.0 ** 30
    for r in range(N):
        for lo in (0, H):
            e = lo + rng.permutation(H)
            for i in range(16): x[r][:, e[2 * i:2 * i + 2]] = (u[:, rng.integers(128)] * (0.5 if i % 2 else -0.5))[:, None]
    w = np.zeros((N, 128, 4, 128, 4), np.float32)
    i = np.arange(128)
    for b in range(4): w[:, i, b, i, b] = 1
    c, p = packed(w.reshape(N, 128, 2048).astype(BF), rng)
    return {"x": x.astype(np.float32).reshape(N, 128, 4 * C).astype(BF), "u": same(u.astype(np.float32).reshape(128, 512).astype(BF)), "v": d["v"], "wc": c, "ws": p, **factors(odd(rng))}
def setup_inputs_copies(rng):
    d = numbers_of(rng)
    x = d["x"].reshape(N, 128, C, 4)
    s, o = int(rng.integers(N)), rng.permutation(N)
    for r in range(N):
        for h in range(2):
            if r == s and h == 0: continue
            i = H * h + rng.permutation(H)[:[2, 16, H // 2, H][(o[r] + h) % 4]]
            x[r][:, i] = x[r][:, i[:1]]
    x[(s + 1) % N, :, H:] = x[s, :, :H]
    x[(s + 2) % N, :, :H] = 0
    x[(s + 3) % N, :, H:] = 0
    return {"x": x.reshape(N, 128, 4 * C), "u": d["u"], "v": d["v"], **weights(rng), **factors(odd(rng))}
def setup_inputs_spread(rng):
    d = setup_inputs(rng)
    d["x"] = big(wide(rng, N, 128, 4 * C, cols=6))
    d["hc"] = factors(rng.integers(1, 256, 3))["hc"]
    return d
def check_inputs(d):
    b = []
    for k in ("x", "u", "v"):
        a = np.abs(d[k].astype(np.float32))
        if not (np.isfinite(a).all() and ((a == 0) | (a >= 2.0 ** -30) & (a <= 2.0 ** 30)).all()): b.append("a value of " + k)
    if (d["u"] != d["u"][:1]).any(): b.append("u: not the same on all ranks")
    if (d["hc"] != d["hc"][:1, :1]).any(): b.append("hc: not the same in all rows and on all ranks")
    if ((d["hc"] < 1) | (d["hc"] > 255)).any(): b.append("hc: out of range")
    none, least, most = [emit(mx_ref.quantize(np.full((128, 16), k, np.float32).astype(BF)))[1][0, 0] for k in (0.0, 2.0 ** -30, 2.0 ** 30)]
    for r in range(N):
        if ((d["wc"][r] == 0x7F) | (d["wc"][r] == 0xFF)).any(): b.append("wc: a code that is no number")
        s = mx_ref.live(d["ws"][r])
        if ((s != none) & ((s < least) | (s > most))).any(): b.append("ws: a scale out of range")
        c = d["wc"][r].reshape(128, -1, 4)
        if ((c != 0) & (c != 0x80) & np.repeat(s == none, 8, axis=0)[:, :, None]).any(): b.append("wc: a number under the scale of zeros")
    return b
def reference(x, u, v, wc, ws, hc):
    qu = [mx_ref.quantize(u[r]) for r in range(N)]
    lay = [pk(wc[r], ws[r]) for r in range(N)]
    now = [x[r] for r in range(N)]
    for t in range(R):
        w = H * (t % 2)
        o = H - w
        num, adr, came = [], [], []
        for r in range(N):
            q = mx_ref.quantize(now[r])
            d = decode(q).astype(BF)
            a = addresses(mx_ref.matmul(qu[r], q), hc[r][0])
            z = written(np.ascontiguousarray(d[:, 4 * w:4 * w + 4 * H]), a[:, :, w:w + H])
            came.append(decode(mx_ref.quantize(z)).astype(BF))
            num.append(d)
            adr.append(a)
        for r in range(N):
            e = [gcols(came[(r - 1) % N], adr[r][:, k, o:o + H]).astype(np.float32) for k in range(3)]
            q = mx_ref.quantize(((e[0] + e[1]) + e[2]).astype(BF))
            new = now[r].copy()
            new[:, 4 * o:4 * o + 4 * H] = tile([mx_ref.matmul(pick(lay[r], np.arange(128 * b, 128 * b + 128)), q) * np.float32(0.015625) + num[r][:, 4 * o + b:4 * o + 4 * H:4].astype(np.float32) for b in range(4)])
            now[r] = new
    y = np.zeros((N, 128, C), np.float32)
    oc, osc = np.zeros((N, 128, 4 * C), np.uint8), np.zeros((N, 16, C), np.uint8)
    for r in range(N):
        q = mx_ref.quantize(now[r])
        y[r] = mx_ref.matmul(mx_ref.quantize(v[r]), q)
        oc[r], osc[r] = emit(q)
    return {"y": y, "oc": oc, "osc": osc}

@@ -1,0 +1,435 @@
+import math
+from concourse.mybir import dt, AluOpType as Op, ActivationFunctionType as Act
+
+X4, U8, BF, F32, I32, U16 = "float8_e4m3fn_x4", "uint8", "bfloat16", "float32", "int32", "uint16"
+SCRATCH = {}
+for _n, _w in dict(a0=128, a1=128, b1=128, fin=256, l0=128, l1=128, l2=128, uu=128, vv=128, ww=512, ee=512, e6=512,
+                   kb=256, sg=128, fl=128, nn=128, ff=128).items():
+    SCRATCH["q" + _n] = ("sbuf", [128, _w], X4)
+    SCRATCH["s" + _n] = ("sbuf", [128, _w], U8)
+for _k, _d in (
+        (BF, dict(x0=512, x1=512, ut=512, vt=512, et=2048, et6=2048, kbt=1024, sgt=512, flt=512, nt=512, ft=512,
+                  xn=512, ids=128, gm=128, t16=128, bk=256, pw=4, tab=64, rst=128, gw=432, gx=384, ow=384, tw=576,
+                  mw=576, ew=576, za=512, og=256, rg=384, sel=384, cx=256, eye=128, hb=24, sn=72, m96=96, pp=48,
+                  osn=256, rsn=384)),
+        (F32, dict(pf32=8, t4=32, sel4=32, dx=64, mul=64, hcf=4, ks=32, xs=384, y1=96, tt=512, yo=256)),
+        (I32, dict(pi=8, c16=8, iw=8, dump=8, pk=12, nhb=24, hci=4, pr=24, hh=24, nh=24, rn=24, n1=64, n2=64, n3=32,
+                   n4=16, y3=24, aa=72, m12=16, mmx=16, rr=24, r2=24, v2=24, own=8, ee2=16, dd=16, t2=16, hab=16)),
+        (U16, dict(upk=4, urep=6, uh=24, urn=24, uidx=8, uown=8, uhab=16, uo=16, urd=24))):
+    for _n, _w in _d.items():
+        SCRATCH[_n] = ("sbuf", [128, _w], _k)
+for _n in range(8):
+    SCRATCH["ps%d" % _n] = ("psum", [128, 512], F32)
+
+_DMAS = ["x0", "x1", "u", "v", "hc", "wc", "ws"] + ["%s%d" % (_n, _h) for _h in range(2) for _n in ("y", "oc", "sa", "sb", "sc", "sd")]
+SEMAPHORES = ["V", "S", "P", "G"] + ["d_" + _n for _n in _DMAS] + ["arr%d" % _t for _t in range(3)] + ["left%d" % _t for _t in range(3)]
+
+SLOT = (0, 2, 1)
+LN2 = math.log(2.0)
+
+
+def rank_program(g, core, T, topo):
+    rank = T.rank_of(core)
+    if rank is None:
+        return
+    nxt = T.cores[(rank + 1) % len(T.cores)]
+    rid, pid, _se = topo.addr(nxt)
+    mask = topo.mask(core, nxt)
+    n_eng = len(topo.engines(core, nxt))
+    n_in = len(topo.engines(T.cores[rank - 1], core))
+
+    eng = {"V": g.vector, "S": g.scalar, "P": g.tensor, "G": g, "Y": g.sync}
+    total = {}
+    clock = {q: {} for q in eng}
+    hist = {}
+
+    def A(name, lo=0, hi=None, step=1):
+        if hi is None:
+            hi = SCRATCH[name][1][1]
+        ap = T[name][:, lo:hi] if step == 1 else T[name][:, lo:hi:step]
+        return (ap, [(name, lo, hi, step)])
+
+    def IND(win, off):
+        return (win[0].indirect(off[0]), win[1] + off[1])
+
+    def meets(a, b):
+        if a[0].startswith("ps"):
+            return True
+        if a[2] <= b[1] or b[2] <= a[1]:
+            return False
+        return not (a[3] == b[3] and a[3] > 1 and (a[1] - b[1]) % a[3] != 0)
+
+    def wait(q, ev):
+        sem, val, snap = ev
+        if clock[q].get(sem, 0) >= val:
+            return
+        eng[q].wait_ge(T.sem[sem], val)
+        for k, x in snap.items():
+            if clock[q].get(k, 0) < x:
+                clock[q][k] = x
+        clock[q][sem] = val
+
+    def before(q, writes, reads, chain=False):
+        need = []
+        for regs, w in ((writes, True), (reads, False)):
+            for r in regs:
+                for (o, ow, ev) in hist.get(r[0], []):
+                    if (w or ow or r[0].startswith("ps")) and meets(r, o):
+                        if chain and r[0].startswith("ps") and ev[0] == "P":
+                            continue
+                        need.append(ev)
+        need.sort(key=lambda e: -e[1])
+        for ev in need:
+            wait(q, ev)
+
+    def after(ev, writes, reads):
+        for r in writes:
+            hist.setdefault(r[0], []).append((r, True, ev))
+        for r in reads:
+            hist.setdefault(r[0], []).append((r, False, ev))
+
+    def regs(xs):
+        return [r for x in xs if isinstance(x, tuple) for r in x[1]]
+
+    def ap(x):
+        return x[0] if isinstance(x, tuple) else x
+
+    def run(q, make, outs, ins, chain=False):
+        w, r = regs(outs), regs(ins)
+        before(q, w, r, chain)
+        total[q] = total.get(q, 0) + 1
+        make().then_inc(T.sem[q], 1)
+        after((q, total[q], dict(clock[q])), w, r)
+
+    def dma(q, name, out, in_):
+        w, r = regs([out]), regs([in_])
+        before(q, w, r)
+        sem = "d_" + name
+        total[sem] = 16
+        eng[q].dma_start(ap(out), ap(in_)).then_inc(T.sem[sem], 16)
+        after((sem, 16, dict(clock[q])), w, r)
+
+    def by(x):
+        return (x[0].bitcast(dt.uint8), x[1])
+
+    V = g.vector
+
+    def cp(o, i, scatter=None):
+        if scatter is None:
+            run("V", lambda: V.tensor_copy(o[0], i[0]), [o], [i])
+        else:
+            run("V", lambda: V.tensor_copy(o[0].indirect(scatter[0]), i[0]), [o], [i, scatter])
+
+    def tt(o, a, b, op):
+        run("V", lambda: V.tensor_tensor(o[0], a[0], b[0], op), [o], [a, b])
+
+    def ts(o, a, s1, op0, s2=None, op1=None):
+        if op1 is None:
+            run("V", lambda: V.tensor_scalar(o[0], a[0], ap(s1), None, op0), [o], [a, s1])
+        else:
+            run("V", lambda: V.tensor_scalar(o[0], a[0], ap(s1), ap(s2), op0, op1), [o], [a, s1, s2])
+
+    def scan(o, a, b, init, op0, op1):
+        run("V", lambda: V.tensor_tensor_scan(o[0], a[0], b[0], init, op0, op1), [o], [a, b])
+
+    def fill(o, c):
+        run("V", lambda: V.memset(o[0], c), [o], [])
+
+    def act(o, i, func=Act.Copy, bias=None, scale=1.0):
+        if bias is None:
+            run("S", lambda: g.scalar.activation(o[0], i[0], func, scale=scale), [o], [i])
+        else:
+            run("S", lambda: g.scalar.activation(o[0], i[0], func, bias=bias, scale=scale), [o], [i])
+
+    def iota(o, pattern, base, mult=0):
+        if SCRATCH[o[1][0][0]][2] == I32:
+            run("G", lambda: g.iota(o[0], pattern, base, mult), [o], [])
+        else:
+            run("G", lambda: g.iota(o[0], pattern, base, mult, allow_small_or_imprecise_dtypes=True), [o], [])
+
+    def M(name, lo=0, hi=None):
+        return (A("q" + name, lo, hi), A("s" + name, lo, hi))
+
+    def quant(m, t):
+        run("V", lambda: V.quantize_mx(m[0][0], m[1][0], t[0]), [m[0], m[1]], [t])
+
+    def mm(bank, w, x, start=True, stop=True):
+        o = A("ps%d" % bank, 0, 128)
+        run("P", lambda: g.tensor.matmul_mx(o[0], w[0][0], w[1][0], x[0][0], x[1][0], start, stop),
+            [o], [w[0], w[1], x[0], x[1]], chain=not start)
+
+    def send(t, m):
+        land = M("l%d" % t)
+        before("G", [], m[0][1] + m[1][1])
+        arr, left = "arr%d" % t, "left%d" % t
+        g.remote_dma(by(land[0])[0], by(m[0])[0], T.sem[arr], T.sem[left], pid, rid, mask)
+        g.remote_dma(land[1][0], m[1][0], T.sem[arr], T.sem[left], pid, rid, mask)
+        total[arr], total[left] = 2 * n_in, 2 * n_eng
+        after((left, 2 * n_eng, dict(clock["G"])), [], m[0][1] + m[1][1])
+        after((arr, 2 * n_in, {}), land[0][1] + land[1][1], [])
+
+    def PS(b, n=128):
+        return A("ps%d" % b, 0, n)
+
+    def plane(name, b):
+        return A(name, 128 * b, 128 * b + 128)
+
+    def window(name, b, n=144):
+        return A(name, 144 * b, 144 * b + n)
+
+    dma("Y", "x0", A("x0"), T.x[:, 0:512])
+    dma("S", "u", A("ut"), T.u[:])
+    dma("Y", "x1", A("x1"), T.x[:, 512:1024])
+    dma("Y", "hc", A("hci", 0, 3), T.hc[:])
+    dma("Y", "wc", by(A("qww")), T.wc[:])
+    dma("Y", "ws", A("sww"), T.ws[:])
+    dma("Y", "v", A("vt"), T.v[:])
+
+    iota(A("pi", 0, 1), [[0, 1]], 0, 1)
+    iota(A("ids"), [[1, 128]], 0)
+    iota(A("t16"), [[0, 8], [1, 16]], 0)
+    iota(A("gm"), [[1, 8], [0, 16]], 0)
+    iota(A("t4"), [[0, 8], [1, 4]], 0)
+    iota(A("c16"), [[16, 8]], 0)
+    iota(A("pk", 0, 4), [[32, 4]], 31)
+    iota(A("pk", 4, 10), [[4, 3], [0, 2]], 0)
+    pfl, jf, gf, af, bf_, kf = [A("pf32", i, i + 1) for i in range(6)]
+    fill(A("sgt"), 0.0)
+    ts(A("pi", 1, 2), A("pi", 0, 1), 15, Op.bitwise_and)
+    ts(A("pi", 2, 3), A("pi", 0, 1), 4, Op.arith_shift_right)
+    ts(A("pi", 3, 4), A("pi", 0, 1), 2, Op.arith_shift_right, 3, Op.bitwise_and)
+    ts(A("pi", 4, 5), A("pi", 0, 1), 3, Op.bitwise_and)
+    cp(A("pf32", 0, 5), A("pi", 0, 5))
+    act(A("pw", 0, 1), jf, Act.Exp, None, LN2)
+    act(A("pw", 1, 2), jf, Act.Exp, 15 * LN2, -LN2)
+    act(A("pf32", 6, 8), A("pw", 0, 2))
+    ts(A("eye"), A("ids"), pfl, Op.is_equal)
+    fill(A("kbt"), 0.0)
+    for b in range(4):
+        for t in range(4):
+            act(A("et", 512 * b + t, 512 * b + 512, 4), A("eye"), Act.Copy, None, float(t == b))
+    for b in range(4):
+        act(A("et6", 512 * b, 512 * b + 512), A("et", 512 * b, 512 * b + 512), Act.Copy, None, 64.0)
+
+    def selector(out, pos, col, big, period, n, tmp):
+        ts(A(tmp, 0, n), A(pos, 0, n), col, Op.is_equal, big, Op.mult)
+        ts(A(tmp, n, 2 * n), A(pos, 0, n), col, Op.is_lt, -2.0 * big, Op.mult)
+        tt(A(out, 0, n), A(tmp, 0, n), A(tmp, n, 2 * n), Op.add)
+        ts(A(out, period - 1, n, period), A(out, period - 1, n, period), -2.0 * big, Op.add)
+
+    for f in range(4):
+        ts(A("tab", 16 * f, 16 * f + 16), A("t16", 0, 16), jf, Op.is_equal, 2.0 ** (6 * f), Op.mult)
+    selector("sel4", "t4", af, 65536.0, 4, 32, "dx")
+    quant(M("a0"), A("x0"))
+    send(0, M("a0"))
+    for s in range(3):
+        iota(A("nhb", 8 * s, 8 * s + 8), [[0, 8]], 255 - 64 * SLOT[s])
+    iota(A("flt"), [[0, 512]], 0)
+    for name, n in (("gw", 3), ("tw", 4), ("mw", 4), ("ew", 4)):
+        for b in range(n):
+            iota(A(name, 144 * b + 128, 144 * b + 144), [[0, 16]], 0)
+    quant(M("uu"), A("ut"))
+    quant(M("a1"), A("x1"))
+    for i in range(2):
+        ts(plane("bk", i), A("gm"), gf, Op.is_equal, A("pf32", 6 + i, 7 + i), Op.mult)
+    for t in range(4):
+        cp(A("kbt", 5 * t, 512, 16), A("bk", t, 128, 4))
+    cp(A("kbt", 512, 1024, 4), plane("bk", 1))
+    cp(A("hcf", 0, 3), A("hci", 0, 3))
+    quant(M("kb"), A("kbt"))
+    KW, BW = M("kb", 0, 128), M("kb", 128, 256)
+
+    def nothing():
+        return None
+
+    def addresses(q, after_keys=nothing):
+        mm(4, M("uu"), q)
+        ts(A("sgt", 0, 128), PS(4), 0.0, Op.is_gt)
+        quant(M("sg"), A("sgt"))
+        mm(5, KW, M("sg"))
+        after_keys()
+        scan(A("ks"), PS(5, 32), A("sel4"), -65536.0, Op.max, Op.add)
+        for s in range(3):
+            k = SLOT[s]
+            ts(A("pr", 8 * s, 8 * s + 8), A("ks", 3, 32, 4), 65536.0, Op.add, A("hcf", k, k + 1), Op.mult)
+        ts(A("hh"), A("pr"), 8, Op.arith_shift_right, 63, Op.bitwise_and)
+
+    def lists_a():
+        fill(A("rst"), 1.0)
+        ts(A("iw"), A("c16"), jf, Op.add)
+        ts(kf, af, 2.0, Op.min, 128.0, Op.mult)
+        fill(A("rst", 0, 128, 32), 0.0)
+
+    def more_constants():
+        ts(A("dump"), A("iw"), 256.0, Op.add)
+        ts(A("upk"), A("pk", 0, 4), kf, Op.add)
+        ts(A("urep"), A("pk", 4, 10), bf_, Op.add)
+        for f in range(4):
+            fill(A("mul", f, 64, 4), 2.0 ** (-6 * f))
+        fill(A("m96", 3, 96, 4), -1.0)
+        quant(M("ee"), A("et"))
+        selector("sel", "t16", jf, 256.0, 16, 128, "cx")
+        cp(plane("sel", 1), plane("sel", 0))
+        cp(plane("sel", 2), plane("sel", 0))
+
+    def outputs(h, qa, qb):
+        q = M("fin", 128 * h, 128 * h + 128)
+        mm(6, M("vv"), q)
+        dma(qa, "oc%d" % h, T.oc[:, 512 * h:512 * h + 512], by(q[0]))
+        for i in range(4):
+            dma((qb, qa)[i % 2], "s%s%d" % ("abcd"[i], h), T.osc[4 * i:4 * i + 4, 128 * h:128 * h + 128],
+                (T.sfin[32 * i:32 * i + 4, 128 * h:128 * h + 128], q[1][1]))
+        cp(plane("yo", h), PS(6))
+        dma(qb, "y%d" % h, T.y[:, 128 * h:128 * h + 128], plane("yo", h))
+
+    E = [M("ee", 128 * b, 128 * b + 128) for b in range(4)]
+    E6 = [M("e6", 128 * b, 128 * b + 128) for b in range(4)]
+    readers = [M("a1"), M("a0"), M("b1")]
+    made = [M("b1"), M("fin", 0, 128), M("fin", 128, 256)]
+    S6 = 0.015625
+
+    for t in range(3):
+        addresses(readers[t], lists_a if t == 0 else nothing)
+        tt(A("rn"), A("nhb"), A("hh"), Op.subtract)
+        fill(A("ow"), 128.0)
+        cp(A("urn"), A("rn"))
+        if t == 0:
+            more_constants()
+        if t == 1:
+            quant(M("vv"), A("vt"))
+        if t == 2:
+            outputs(0, "Y", "Y")
+        land = M("l%d" % t)
+
+        def scaled(b):
+            if t == 0:
+                quant(E6[b], A("et6", 512 * b, 512 * b + 512))
+
+        def unpack():
+            for b in range(4):
+                mm(b, E[b], land)
+            scaled(0)
+
+        addresses(land, unpack)
+        cp(A("uh"), A("hh"))
+
+        for p in range(3):
+            if p == 0:
+                src = [IND(A("tab"), A("uh", 8 * s, 8 * s + 8)) for s in range(3)]
+                dst = [window("gw", s, 128) for s in range(3)]
+            else:
+                src = [IND(window("gw", s), A("uidx")) for s in range(3)]
+                dst = [plane("gx", s) for s in range(3)]
+            act(dst[1], src[1])
+            act(dst[2], src[2])
+            cp(dst[0], src[0])
+            for s in range(3):
+                scan(plane("xs", s), A("rst"), dst[s], 0.0, Op.mult, Op.add)
+                if p == 0 and s == 1:
+                    ts(A("hb"), A("hh"), 1.0625, Op.mult, 159.53, Op.add)
+                    for f in range(3):
+                        act(A("sn", 24 * f, 24 * f + 24), A("hb"), Act.Sign, 175.5 + 17 * f, -1.0)
+                    act(A("pp", 0, 24), A("hb"), Act.Exp, -211 * LN2, LN2)
+                    for f in range(3):
+                        act(A("m96", f, 96, 4), A("sn", 24 * f, 24 * f + 24), Act.Relu, None, 2.0 ** 17)
+                    act(A("pp", 24, 48), A("pp", 0, 24), Act.Copy, None, -1.0)
+                    for b in range(4):
+                        act(window("tw", b, 128), PS(b))
+                    act(plane("za", 0), PS(0))
+            tt(A("n1"), IND(A("xs"), A("upk")), A("mul"), Op.mult)
+            ts(A("n2"), A("n1"), 63, Op.bitwise_and)
+            tt(A("n3"), A("n2", 0, 32), A("n2", 32, 64), Op.add)
+            tt(A("n4"), A("n3", 0, 16), A("n3", 16, 32), Op.add)
+            ts(A("flt", 0, 384, 4), IND(A("n4"), A("urep")), 1.0, Op.is_equal, A("hb", 0, 1), Op.min)
+            quant(M("fl"), A("flt"))
+            mm(6, BW, M("fl"))
+            if p == 0:
+                tt(A("nh"), A("nhb"), A("hh"), Op.subtract)
+            if p == 1:
+                tt(A("dd", 0, 8), A("nh", 16, 24), A("nh", 0, 8), Op.subtract)
+                tt(A("dd", 8, 16), A("nh", 16, 24), A("nh", 8, 16), Op.subtract)
+            if p == 2:
+                tt(A("rr"), A("aa", 0, 24), A("aa", 24, 48), Op.max)
+            scaled(p + 1)
+            scan(A("y1"), PS(6, 96), A("m96"), 0.0, Op.max, Op.mult)
+            tt(A("y3"), A("y1", 3, 96, 4), A("pp", 24, 48), Op.mult)
+            a = 24 * p
+            ts(A("aa", a, a + 24), A("y3"), 4 + p, Op.arith_shift_right, 2048 >> p, Op.bitwise_and)
+            if p < 2:
+                tt(A("m12", 0, 8), A("aa", a, a + 8), A("aa", a + 8, a + 16), Op.max)
+                tt(A("m12", 8, 16), A("aa", a + 16, a + 24), (A("iw"), A("mmx", 0, 8))[p], Op.max)
+                tt(A("mmx", 8 * p, 8 * p + 8), A("m12", 0, 8), A("m12", 8, 16), Op.max)
+                ts(A("uidx"), A("mmx", 8 * p, 8 * p + 8), 128.0, Op.min)
+
+        tt(A("r2"), A("aa", 48, 72), A("rr"), Op.max)
+        tt(A("v2"), A("r2"), A("nh"), Op.add)
+        tt(A("m12", 0, 8), A("v2", 0, 8), A("v2", 8, 16), Op.max)
+        tt(A("m12", 8, 16), A("v2", 16, 24), A("dump"), Op.max)
+        tt(A("mmx", 0, 8), A("m12", 0, 8), A("m12", 8, 16), Op.max)
+        ts(A("own"), A("mmx", 0, 8), 511, Op.bitwise_and)
+        ts(A("ee2", 0, 8), A("own"), 192.0, Op.is_ge)
+        ts(A("ee2", 8, 16), A("own"), 128.0, Op.is_lt)
+        cp(A("uown"), A("own"))
+        tt(A("t2"), A("ee2"), A("dd"), Op.mult)
+        cp(A("ow"), A("ids"), A("uown"))
+        tt(A("hab"), A("nh", 0, 16), A("t2"), Op.add)
+        cp(A("uhab"), A("hab"))
+        act(plane("og", 1), IND(A("ow"), A("uhab", 8, 16)))
+        cp(plane("og", 0), IND(A("ow"), A("uhab", 0, 8)))
+        act(plane("rg", 0), IND(A("ow"), A("urn", 0, 8)))
+        scan(A("osn"), A("og"), A("sel", 0, 256), -256.0, Op.max, Op.add)
+        ts(A("uo"), A("osn", 15, 256, 16), 256.0, Op.add)
+        oa, ob = A("uo", 0, 8), A("uo", 8, 16)
+
+        for b in range(1, 4):
+            act(plane("za", b), IND(window("tw", b), oa))
+        act(plane("rg", 1), IND(A("ow"), A("urn", 8, 16)))
+        tt(plane("tt", 0), IND(window("tw", 0), oa), plane("za", 0), Op.subtract)
+        tt(plane("tt", 1), PS(1), plane("za", 1), Op.subtract)
+        tt(window("mw", 0, 128), IND(window("tw", 0), ob), plane("tt", 0), Op.add)
+        act(plane("za", 0), IND(window("mw", 0), oa))
+        for b in range(1, 4):
+            if b < 3:
+                tt(plane("tt", b + 1), PS(b + 1), plane("za", b + 1), Op.subtract)
+            else:
+                tt(plane("tt", 0), PS(0), plane("za", 0), Op.add)
+            tt(window("mw", b, 128), IND(window("tw", b), ob), plane("tt", b), Op.subtract)
+            act(plane("za", b), IND(window("mw", b), oa))
+        act(plane("rg", 2), IND(A("ow"), A("urn", 16, 24)))
+        for b in range(4):
+            if b < 3:
+                tt(plane("tt", b + 1), PS(b + 1), plane("za", b + 1), Op.add)
+            tt(A("nt", b, 512, 4), IND(window("mw", b), ob), plane("tt", b), Op.add)
+        quant(M("nn"), A("nt"))
+        for b in range(4):
+            mm(4 + b, E[b], M("nn"))
+        for b in range(4):
+            mm(b, E6[b], readers[t], True, False)
+        scan(A("rsn"), A("rg"), A("sel"), -256.0, Op.max, Op.add)
+        ts(A("urd"), A("rsn", 15, 384, 16), 256.0, Op.add)
+
+        act(window("ew", 0, 128), PS(4))
+        cp(window("ew", 1, 128), PS(5))
+        cp(window("ew", 2, 128), PS(6))
+        for b in range(4):
+            if b == 2:
+                act(window("ew", 3, 128), PS(7))
+            act(plane("za", b), IND(window("ew", b), A("urd", 0, 8)))
+        for b in range(5):
+            if b < 4:
+                tt(plane("tt", b), IND(window("ew", b), A("urd", 16, 24)), plane("za", b), Op.add)
+            if b > 0:
+                tt(A("ft", b - 1, 512, 4), IND(window("ew", b - 1), A("urd", 8, 16)), plane("tt", b - 1), Op.add)
+        quant(M("ff"), A("ft"))
+        for b in (0, 2, 1, 3):
+            mm(b, M("ww", 128 * b, 128 * b + 128), M("ff"), False, True)
+        for b in range(2):
+            ts(A("xn", b, 512, 4), PS(b), S6, Op.mult)
+            act(A("xn", b + 2, 512, 4), PS(b + 2), Act.Copy, None, S6)
+        quant(made[t], A("xn"))
+        if t < 2:
+            send(t + 1, made[t])
+
+    outputs(1, "Y", "S")
+    for sem, val in total.items():
+        wait("G", (sem, val, {}))

@@ -1,5 +1,5 @@
 import math
-from concourse.mybir import dt, AluOpType as Op, ActivationFunctionType as Act
+from concourse.mybir import dt, AluOpType as Op, ActivationFunctionType as Act, AxisListType
 
 X4, U8, BF, F32, I32, U16 = "float8_e4m3fn_x4", "uint8", "bfloat16", "float32", "int32", "uint16"
 SCRATCH = {}
@@ -9,13 +9,13 @@ for _n, _w in dict(a0=128, a1=128, b1=128, fin=256, l0=128, l1=128, l2=128, uu=1
     SCRATCH["s" + _n] = ("sbuf", [128, _w], U8)
 for _k, _d in (
         (BF, dict(x0=512, x1=512, ut=512, vt=512, et=2048, et6=2048, kbt=1024, sgt=512, flt=512, nt=512, ft=512,
-                  xn=512, ids=128, gm=128, t16=128, bk=256, pw=4, tab=64, rst=128, gw=432, gx=384, ow=384, tw=576,
-                  mw=576, ew=576, za=512, og=256, rg=384, sel=384, cx=256, eye=128, hb=24, sn=72, m96=96, pp=48,
-                  osn=256, rsn=384)),
-        (F32, dict(pf32=8, t4=32, sel4=32, dx=64, mul=64, hcf=4, ks=32, xs=384, y1=96, tt=512, yo=256)),
-        (I32, dict(pi=8, c16=8, iw=8, dump=8, pk=12, nhb=24, hci=4, pr=24, hh=24, nh=24, rn=24, n1=64, n2=64, n3=32,
-                   n4=16, y3=24, aa=72, m12=16, mmx=16, rr=24, r2=24, v2=24, own=8, ee2=16, dd=16, t2=16, hab=16)),
-        (U16, dict(upk=4, urep=6, uh=24, urn=24, uidx=8, uown=8, uhab=16, uo=16, urd=24))):
+                  xn=512, ids=128, gm=128, t16=128, bk=256, pw=4, tab=64, gw=432, gx=384, ow=384, tw=576,
+                  mw=576, ew=576, za=512, og=256, rg=384, sel=384, cx=256, eye=128, hb=24, sn=72, pp=24,
+                  osn=256, rsn=384, gy=128, gj=256)),
+        (F32, dict(pf32=10, t4=32, sel4=32, dx=64, mul=16, hcf=4, ks=32, xs=8, y1=96, tt=512, yo=256, m96=96,
+                   yr=24, sd=40, sv=40, cur=40, lf=8, he=32, hv=32, hab=32)),
+        (I32, dict(pi=8, c16=8, iw=8, pk=8, nhb=24, hci=4, pr=24, hh=24, nh=24, rn=24, n1=16, n2=16)),
+        (U16, dict(upk=2, urep=6, uh=24, urn=24, uidx=8, uown=8, uhab=16, uo=16, urd=24))):
     for _n, _w in _d.items():
         SCRATCH[_n] = ("sbuf", [128, _w], _k)
 for _n in range(8):
@@ -25,6 +25,7 @@ _DMAS = ["x0", "x1", "u", "v", "hc", "wc", "ws"] + ["%s%d" % (_n, _h) for _h in 
 SEMAPHORES = ["V", "S", "P", "G"] + ["d_" + _n for _n in _DMAS] + ["arr%d" % _t for _t in range(3)] + ["left%d" % _t for _t in range(3)]
 
 SLOT = (0, 2, 1)
+PLACE = (3, 1, 2)
 LN2 = math.log(2.0)
 
 
@@ -132,11 +133,16 @@ def rank_program(g, core, T, topo):
     def scan(o, a, b, init, op0, op1):
         run("V", lambda: V.tensor_tensor_scan(o[0], a[0], b[0], init, op0, op1), [o], [a, b])
 
+    def total_of(o, i):
+        run("V", lambda: V.tensor_reduce(o[0], i[0], AxisListType.X, Op.add), [o], [i])
+
     def fill(o, c):
         run("V", lambda: V.memset(o[0], c), [o], [])
 
-    def act(o, i, func=Act.Copy, bias=None, scale=1.0):
-        if bias is None:
+    def act(o, i, func=Act.Copy, bias=None, scale=1.0, acc=None):
+        if acc is not None:
+            run("S", lambda: g.scalar.activation(o[0], i[0], func, scale=scale, accum_out=acc[0]), [o, acc], [i])
+        elif bias is None:
             run("S", lambda: g.scalar.activation(o[0], i[0], func, scale=scale), [o], [i])
         else:
             run("S", lambda: g.scalar.activation(o[0], i[0], func, bias=bias, scale=scale), [o], [i])
@@ -177,6 +183,12 @@ def rank_program(g, core, T, topo):
     def window(name, b, n=144):
         return A(name, 144 * b, 144 * b + n)
 
+    def third(name, s):
+        return A(name, 8 * s, 8 * s + 8)
+
+    def col(name, i):
+        return A(name, i, i + 1)
+
     dma("Y", "x0", A("x0"), T.x[:, 0:512])
     dma("S", "u", A("ut"), T.u[:])
     dma("Y", "x1", A("x1"), T.x[:, 512:1024])
@@ -187,43 +199,52 @@ def rank_program(g, core, T, topo):
 
     iota(A("pi", 0, 1), [[0, 1]], 0, 1)
     iota(A("ids"), [[1, 128]], 0)
+    iota(A("t4"), [[0, 8], [1, 4]], 0)
     iota(A("t16"), [[0, 8], [1, 16]], 0)
     iota(A("gm"), [[1, 8], [0, 16]], 0)
-    iota(A("t4"), [[0, 8], [1, 4]], 0)
     iota(A("c16"), [[16, 8]], 0)
-    iota(A("pk", 0, 4), [[32, 4]], 31)
-    iota(A("pk", 4, 10), [[4, 3], [0, 2]], 0)
-    pfl, jf, gf, af, bf_, kf = [A("pf32", i, i + 1) for i in range(6)]
+    iota(A("pk", 0, 6), [[4, 3], [0, 2]], 0)
+    pfl, jf, gf, af, bf_, kf = [col("pf32", i) for i in range(6)]
     fill(A("sgt"), 0.0)
-    ts(A("pi", 1, 2), A("pi", 0, 1), 15, Op.bitwise_and)
-    ts(A("pi", 2, 3), A("pi", 0, 1), 4, Op.arith_shift_right)
-    ts(A("pi", 3, 4), A("pi", 0, 1), 2, Op.arith_shift_right, 3, Op.bitwise_and)
-    ts(A("pi", 4, 5), A("pi", 0, 1), 3, Op.bitwise_and)
+    ts(col("pi", 1), col("pi", 0), 15, Op.bitwise_and)
+    ts(col("pi", 2), col("pi", 0), 4, Op.arith_shift_right)
+    ts(col("pi", 3), col("pi", 0), 2, Op.arith_shift_right, 3, Op.bitwise_and)
+    ts(col("pi", 4), col("pi", 0), 3, Op.bitwise_and)
+    fill(A("xs"), 0.0)
+    fill(A("sd"), 0.0)
     cp(A("pf32", 0, 5), A("pi", 0, 5))
-    act(A("pw", 0, 1), jf, Act.Exp, None, LN2)
-    act(A("pw", 1, 2), jf, Act.Exp, 15 * LN2, -LN2)
+    act(col("pw", 0), jf, Act.Exp, None, LN2)
+    act(col("pw", 1), jf, Act.Exp, 15 * LN2, -LN2)
     act(A("pf32", 6, 8), A("pw", 0, 2))
-    ts(A("eye"), A("ids"), pfl, Op.is_equal)
     fill(A("kbt"), 0.0)
+    ts(A("eye"), A("ids"), pfl, Op.is_equal)
     for b in range(4):
         for t in range(4):
             act(A("et", 512 * b + t, 512 * b + 512, 4), A("eye"), Act.Copy, None, float(t == b))
     for b in range(4):
         act(A("et6", 512 * b, 512 * b + 512), A("et", 512 * b, 512 * b + 512), Act.Copy, None, 64.0)
 
-    def selector(out, pos, col, big, period, n, tmp):
-        ts(A(tmp, 0, n), A(pos, 0, n), col, Op.is_equal, big, Op.mult)
-        ts(A(tmp, n, 2 * n), A(pos, 0, n), col, Op.is_lt, -2.0 * big, Op.mult)
-        tt(A(out, 0, n), A(tmp, 0, n), A(tmp, n, 2 * n), Op.add)
-        ts(A(out, period - 1, n, period), A(out, period - 1, n, period), -2.0 * big, Op.add)
+    def selector(out, pos, c, big, period, n, tmp):
+        def first():
+            ts(A(tmp, 0, n), A(pos, 0, n), c, Op.is_equal, big, Op.mult)
+            ts(A(tmp, n, 2 * n), A(pos, 0, n), c, Op.is_lt, -2.0 * big, Op.mult)
+        return [first, lambda: tt(A(out, 0, n), A(tmp, 0, n), A(tmp, n, 2 * n), Op.add),
+                lambda: ts(A(out, period - 1, n, period), A(out, period - 1, n, period), -2.0 * big, Op.add)]
 
+    s4 = selector("sel4", "t4", af, 65536.0, 4, 32, "dx")
+    s16 = selector("sel", "t16", jf, 256.0, 16, 128, "cx")
+    s4[0]()
+    fill(A("he", 0, 32, 2), 0.0)
+    fill(A("sv", 0, 40, 5), 0.0)
+    fill(A("sv", 4, 40, 5), 1024.0)
+    s4[1]()
     for f in range(4):
-        ts(A("tab", 16 * f, 16 * f + 16), A("t16", 0, 16), jf, Op.is_equal, 2.0 ** (6 * f), Op.mult)
-    selector("sel4", "t4", af, 65536.0, 4, 32, "dx")
+        ts(A("tab", 16 * f, 16 * f + 16), A("t16", 0, 16), jf, Op.is_equal, (1.0, 256.0, 65536.0, -2.0 ** -40)[f], Op.mult)
+    s4[2]()
     quant(M("a0"), A("x0"))
     send(0, M("a0"))
     for s in range(3):
-        iota(A("nhb", 8 * s, 8 * s + 8), [[0, 8]], 255 - 64 * SLOT[s])
+        iota(third("nhb", s), [[0, 8]], 383 - 64 * SLOT[s])
     iota(A("flt"), [[0, 512]], 0)
     for name, n in (("gw", 3), ("tw", 4), ("mw", 4), ("ew", 4)):
         for b in range(n):
@@ -231,46 +252,42 @@ def rank_program(g, core, T, topo):
     quant(M("uu"), A("ut"))
     quant(M("a1"), A("x1"))
     for i in range(2):
-        ts(plane("bk", i), A("gm"), gf, Op.is_equal, A("pf32", 6 + i, 7 + i), Op.mult)
+        ts(plane("bk", i), A("gm"), gf, Op.is_equal, col("pf32", 6 + i), Op.mult)
+    cp(A("hcf", 0, 3), A("hci", 0, 3))
+    ts(A("iw"), A("c16"), jf, Op.add)
     for t in range(4):
         cp(A("kbt", 5 * t, 512, 16), A("bk", t, 128, 4))
     cp(A("kbt", 512, 1024, 4), plane("bk", 1))
-    cp(A("hcf", 0, 3), A("hci", 0, 3))
+    ts(kf, af, 2.0, Op.min)
+    ts(col("pf32", 8), bf_, 3.0, Op.is_equal, 4.0, Op.mult)
     quant(M("kb"), A("kbt"))
     KW, BW = M("kb", 0, 128), M("kb", 128, 256)
 
     def nothing():
         return None
 
-    def addresses(q, after_keys=nothing):
+    def addresses(q, a=nothing, b=nothing, c=nothing, d=nothing):
         mm(4, M("uu"), q)
         ts(A("sgt", 0, 128), PS(4), 0.0, Op.is_gt)
+        a()
         quant(M("sg"), A("sgt"))
         mm(5, KW, M("sg"))
-        after_keys()
+        b()
         scan(A("ks"), PS(5, 32), A("sel4"), -65536.0, Op.max, Op.add)
+        c()
         for s in range(3):
-            k = SLOT[s]
-            ts(A("pr", 8 * s, 8 * s + 8), A("ks", 3, 32, 4), 65536.0, Op.add, A("hcf", k, k + 1), Op.mult)
+            ts(third("pr", s), A("ks", 3, 32, 4), 65536.0, Op.add, col("hcf", SLOT[s]), Op.mult)
+        d()
         ts(A("hh"), A("pr"), 8, Op.arith_shift_right, 63, Op.bitwise_and)
 
     def lists_a():
-        fill(A("rst"), 1.0)
-        ts(A("iw"), A("c16"), jf, Op.add)
-        ts(kf, af, 2.0, Op.min, 128.0, Op.mult)
-        fill(A("rst", 0, 128, 32), 0.0)
+        ts(col("upk", 0), col("pf32", 8), kf, Op.add)
+        ts(A("urep"), A("pk", 0, 6), bf_, Op.add)
 
-    def more_constants():
-        ts(A("dump"), A("iw"), 256.0, Op.add)
-        ts(A("upk"), A("pk", 0, 4), kf, Op.add)
-        ts(A("urep"), A("pk", 4, 10), bf_, Op.add)
+    def lists_b():
         for f in range(4):
-            fill(A("mul", f, 64, 4), 2.0 ** (-6 * f))
-        fill(A("m96", 3, 96, 4), -1.0)
-        quant(M("ee"), A("et"))
-        selector("sel", "t16", jf, 256.0, 16, 128, "cx")
-        cp(plane("sel", 1), plane("sel", 0))
-        cp(plane("sel", 2), plane("sel", 0))
+            fill(A("mul", f, 16, 4), (1.0, 2.0 ** -8, 2.0 ** -16, 1.0)[f])
+        s16[0]()
 
     def outputs(h, qa, qb):
         q = M("fin", 128 * h, 128 * h + 128)
@@ -287,16 +304,27 @@ def rank_program(g, core, T, topo):
     readers = [M("a1"), M("a0"), M("b1")]
     made = [M("b1"), M("fin", 0, 128), M("fin", 128, 256)]
     S6 = 0.015625
+    ROUND = 1.5 * 2.0 ** 50
 
     for t in range(3):
-        addresses(readers[t], lists_a if t == 0 else nothing)
-        tt(A("rn"), A("nhb"), A("hh"), Op.subtract)
-        fill(A("ow"), 128.0)
-        cp(A("urn"), A("rn"))
+        def clear():
+            fill(A("ow"), 128.0)
+            cp(A("sd", 4, 40, 5), A("iw"))
+
         if t == 0:
-            more_constants()
+            addresses(readers[t], lists_a, lists_b, s16[1], clear)
+            s16[2]()
+        else:
+            addresses(readers[t], nothing, clear)
+        tt(A("rn"), A("nhb"), A("hh"), Op.subtract)
+        if t == 0:
+            quant(M("ee"), A("et"))
         if t == 1:
             quant(M("vv"), A("vt"))
+        cp(A("urn"), A("rn"))
+        if t == 0:
+            cp(plane("sel", 1), plane("sel", 0))
+            cp(plane("sel", 2), plane("sel", 0))
         if t == 2:
             outputs(0, "Y", "Y")
         land = M("l%d" % t)
@@ -310,70 +338,68 @@ def rank_program(g, core, T, topo):
                 mm(b, E[b], land)
             scaled(0)
 
-        addresses(land, unpack)
+        addresses(land, nothing, unpack)
         cp(A("uh"), A("hh"))
+        ts(A("hb"), A("hh"), 1.0625, Op.mult, 159.53, Op.add)
+        tt(A("nh"), A("nhb"), A("hh"), Op.subtract)
+        ends = A("cur", 4, 40, 5)
 
         for p in range(3):
             if p == 0:
-                src = [IND(A("tab"), A("uh", 8 * s, 8 * s + 8)) for s in range(3)]
+                src = [IND(A("tab"), third("uh", s)) for s in range(3)]
                 dst = [window("gw", s, 128) for s in range(3)]
             else:
                 src = [IND(window("gw", s), A("uidx")) for s in range(3)]
                 dst = [plane("gx", s) for s in range(3)]
-            act(dst[1], src[1])
-            act(dst[2], src[2])
+            for s in (1, 2):
+                act(dst[s], src[s], Act.Copy, None, 1.0, col("xs", s))
+            for s in (1, 2):
+                act(plane("gj", s - 1), dst[s], Act.Relu, None, -2.0 ** 40, col("xs", 4 + s))
             cp(dst[0], src[0])
-            for s in range(3):
-                scan(plane("xs", s), A("rst"), dst[s], 0.0, Op.mult, Op.add)
-                if p == 0 and s == 1:
-                    ts(A("hb"), A("hh"), 1.0625, Op.mult, 159.53, Op.add)
-                    for f in range(3):
-                        act(A("sn", 24 * f, 24 * f + 24), A("hb"), Act.Sign, 175.5 + 17 * f, -1.0)
-                    act(A("pp", 0, 24), A("hb"), Act.Exp, -211 * LN2, LN2)
-                    for f in range(3):
-                        act(A("m96", f, 96, 4), A("sn", 24 * f, 24 * f + 24), Act.Relu, None, 2.0 ** 17)
-                    act(A("pp", 24, 48), A("pp", 0, 24), Act.Copy, None, -1.0)
-                    for b in range(4):
-                        act(window("tw", b, 128), PS(b))
-                    act(plane("za", 0), PS(0))
-            tt(A("n1"), IND(A("xs"), A("upk")), A("mul"), Op.mult)
-            ts(A("n2"), A("n1"), 63, Op.bitwise_and)
-            tt(A("n3"), A("n2", 0, 32), A("n2", 32, 64), Op.add)
-            tt(A("n4"), A("n3", 0, 16), A("n3", 16, 32), Op.add)
-            ts(A("flt", 0, 384, 4), IND(A("n4"), A("urep")), 1.0, Op.is_equal, A("hb", 0, 1), Op.min)
+            if p == 0:
+                for s in range(3):
+                    cp(A("sv", PLACE[s], 40, 5), third("nh", s))
+                for f in range(3):
+                    act(A("sn", 24 * f, 24 * f + 24), A("hb"), Act.Sign, 175.5 + 17 * f, -1.0)
+                act(A("pp"), A("hb"), Act.Exp, -211 * LN2, LN2)
+                for f in range(3):
+                    act(A("m96", f, 96, 4), A("sn", 24 * f, 24 * f + 24), Act.Relu, None, 2.0 ** 17)
+                act(A("m96", 3, 96, 4), A("pp"), Act.Copy, None, -2048.0 * (1.0 + 2.0 ** -18))
+                for b in range(4):
+                    act(window("tw", b, 128), PS(b))
+                act(plane("za", 0), PS(0))
+            else:
+                for s in range(3):
+                    tt(A("m96", 32 * s + 3, 32 * s + 32, 4), A("m96", 32 * s + 3, 32 * s + 32, 4), A("lf"), Op.mult)
+            ts(A("gy"), dst[0], 0.0, Op.is_lt)
+            total_of(col("xs", 0), dst[0])
+            total_of(col("xs", 4), A("gy"))
+            tt(A("n1"), IND(A("xs"), col("upk", 0)), A("mul"), Op.mult)
+            ts(A("n2"), A("n1"), 255, Op.bitwise_and)
+            ts(A("flt", 0, 384, 4), IND(A("n2"), A("urep")), 1.0, Op.is_equal, col("hb", 0), Op.min)
             quant(M("fl"), A("flt"))
             mm(6, BW, M("fl"))
-            if p == 0:
-                tt(A("nh"), A("nhb"), A("hh"), Op.subtract)
             if p == 1:
-                tt(A("dd", 0, 8), A("nh", 16, 24), A("nh", 0, 8), Op.subtract)
-                tt(A("dd", 8, 16), A("nh", 16, 24), A("nh", 8, 16), Op.subtract)
-            if p == 2:
-                tt(A("rr"), A("aa", 0, 24), A("aa", 24, 48), Op.max)
+                tt(A("hv", 0, 16, 2), third("nh", 2), third("nh", 0), Op.subtract)
+                tt(A("hv", 16, 32, 2), third("nh", 2), third("nh", 1), Op.subtract)
+                cp(A("hv", 1, 32, 2), A("nh", 0, 16))
             scaled(p + 1)
             scan(A("y1"), PS(6, 96), A("m96"), 0.0, Op.max, Op.mult)
-            tt(A("y3"), A("y1", 3, 96, 4), A("pp", 24, 48), Op.mult)
-            a = 24 * p
-            ts(A("aa", a, a + 24), A("y3"), 4 + p, Op.arith_shift_right, 2048 >> p, Op.bitwise_and)
+            ts(A("yr"), A("y1", 3, 96, 4), ROUND, Op.add, ROUND, Op.subtract)
+            for s in range(3):
+                tt(A("sd", PLACE[s], 40, 5), A("y1", 32 * s + 3, 32 * s + 32, 4), third("yr", s), Op.subtract)
+            scan(A("cur"), A("sd"), A("sv"), 0.0, Op.max, Op.min)
             if p < 2:
-                tt(A("m12", 0, 8), A("aa", a, a + 8), A("aa", a + 8, a + 16), Op.max)
-                tt(A("m12", 8, 16), A("aa", a + 16, a + 24), (A("iw"), A("mmx", 0, 8))[p], Op.max)
-                tt(A("mmx", 8 * p, 8 * p + 8), A("m12", 0, 8), A("m12", 8, 16), Op.max)
-                ts(A("uidx"), A("mmx", 8 * p, 8 * p + 8), 128.0, Op.min)
+                ts(A("uidx"), ends, 128.0, Op.min)
+                ts(A("lf"), ends, 128.0, Op.is_lt)
+                cp(A("sd", 4, 40, 5), ends)
 
-        tt(A("r2"), A("aa", 48, 72), A("rr"), Op.max)
-        tt(A("v2"), A("r2"), A("nh"), Op.add)
-        tt(A("m12", 0, 8), A("v2", 0, 8), A("v2", 8, 16), Op.max)
-        tt(A("m12", 8, 16), A("v2", 16, 24), A("dump"), Op.max)
-        tt(A("mmx", 0, 8), A("m12", 0, 8), A("m12", 8, 16), Op.max)
-        ts(A("own"), A("mmx", 0, 8), 511, Op.bitwise_and)
-        ts(A("ee2", 0, 8), A("own"), 192.0, Op.is_ge)
-        ts(A("ee2", 8, 16), A("own"), 128.0, Op.is_lt)
-        cp(A("uown"), A("own"))
-        tt(A("t2"), A("ee2"), A("dd"), Op.mult)
+        ts(A("he", 1, 16, 2), ends, 320.0, Op.is_ge)
+        ts(A("he", 17, 32, 2), ends, 256.0, Op.is_lt)
+        cp(A("uown"), ends)
+        scan(A("hab"), A("he"), A("hv"), 0.0, Op.mult, Op.add)
         cp(A("ow"), A("ids"), A("uown"))
-        tt(A("hab"), A("nh", 0, 16), A("t2"), Op.add)
-        cp(A("uhab"), A("hab"))
+        cp(A("uhab"), A("hab", 1, 32, 2))
         act(plane("og", 1), IND(A("ow"), A("uhab", 8, 16)))
         cp(plane("og", 0), IND(A("ow"), A("uhab", 0, 8)))
         act(plane("rg", 0), IND(A("ow"), A("urn", 0, 8)))

@@ -3,26 +3,27 @@ from concourse.mybir import dt, AluOpType as Op, ActivationFunctionType as Act, 
 
 X4, U8, BF, F32, I32, U16 = "float8_e4m3fn_x4", "uint8", "bfloat16", "float32", "int32", "uint16"
 SCRATCH = {}
-for _n, _w in dict(a0=128, a1=128, b1=128, fin=256, l0=128, l1=128, l2=128, uu=128, vv=128, ww=512, ee=512, e6=512,
+for _n, _w in dict(aa=256, b1=128, fin=256, l0=128, l1=128, l2=128, uu=128, vv=128, ww=512, ee=512, e6=512,
                    kb=256, sg=128, fl=128, nn=128, ff=128).items():
     SCRATCH["q" + _n] = ("sbuf", [128, _w], X4)
     SCRATCH["s" + _n] = ("sbuf", [128, _w], U8)
 for _k, _d in (
-        (BF, dict(x0=512, x1=512, ut=512, vt=512, et=2048, et6=2048, kbt=1024, sgt=512, flt=512, nt=512, ft=512,
+        (BF, dict(xx=1024, ut=512, vt=512, et=2048, et6=2048, kbt=1024, sgt=512, flt=512, nt=512, ft=512,
                   xn=512, ids=128, gm=128, t16=128, bk=256, pw=4, tab=64, gw=432, gx=384, ow=384, tw=576,
                   mw=576, ew=576, za=512, og=256, rg=384, sel=384, cx=256, eye=128, hb=24, sn=72, pp=24,
-                  osn=256, rsn=384, gy=128, gj=256)),
-        (F32, dict(pf32=10, t4=32, sel4=32, dx=64, mul=16, hcf=4, ks=32, xs=8, y1=96, tt=512, yo=256, m96=96,
+                  osn=256, rsn=384, gy=128, gj=256, mul=16)),
+        (F32, dict(pf32=10, t4=64, sel4=64, dx=128, hcf=4, ks=64, xs=8, y1=96, tt=512, yo=256, m96=96,
                    yr=24, sd=40, sv=40, cur=40, lf=8, he=32, hv=32, hab=32)),
-        (I32, dict(pi=8, c16=8, iw=8, pk=8, nhb=24, hci=4, pr=24, hh=24, nh=24, rn=24, n1=16, n2=16)),
-        (U16, dict(upk=2, urep=6, uh=24, urn=24, uidx=8, uown=8, uhab=16, uo=16, urd=24))):
+        (I32, dict(pi=8, c16=8, iw=8, pk=8, nhb=24, hci=4, pr=48, hh=48, nh=48, n1=16, n2=16)),
+        (U16, dict(upk=2, urep=6, uh=24, ub=72, lb=72, uidx=8, uown=8, uhab=16, uo=16, urd=24, lo=48, lr=72))):
     for _n, _w in _d.items():
         SCRATCH[_n] = ("sbuf", [128, _w], _k)
 for _n in range(8):
     SCRATCH["ps%d" % _n] = ("psum", [128, 512], F32)
 
 _DMAS = ["x0", "x1", "u", "v", "hc", "wc", "ws"] + ["%s%d" % (_n, _h) for _h in range(2) for _n in ("y", "oc", "sa", "sb", "sc", "sd")]
-SEMAPHORES = ["V", "S", "P", "G"] + ["d_" + _n for _n in _DMAS] + ["arr%d" % _t for _t in range(3)] + ["left%d" % _t for _t in range(3)]
+SEMAPHORES = (["V", "S", "P", "G"] + ["d_" + _n for _n in _DMAS]
+              + ["%s%s%d" % (_a, _n, _t) for _a in ("arr", "left") for _n in "cbor" for _t in range(3)])
 
 SLOT = (0, 2, 1)
 PLACE = (3, 1, 2)
@@ -33,11 +34,7 @@ def rank_program(g, core, T, topo):
     rank = T.rank_of(core)
     if rank is None:
         return
-    nxt = T.cores[(rank + 1) % len(T.cores)]
-    rid, pid, _se = topo.addr(nxt)
-    mask = topo.mask(core, nxt)
-    n_eng = len(topo.engines(core, nxt))
-    n_in = len(topo.engines(T.cores[rank - 1], core))
+    nxt, prv = T.cores[(rank + 1) % len(T.cores)], T.cores[rank - 1]
 
     eng = {"V": g.vector, "S": g.scalar, "P": g.tensor, "G": g, "Y": g.sync}
     total = {}
@@ -159,20 +156,28 @@ def rank_program(g, core, T, topo):
     def quant(m, t):
         run("V", lambda: V.quantize_mx(m[0][0], m[1][0], t[0]), [m[0], m[1]], [t])
 
-    def mm(bank, w, x, start=True, stop=True):
-        o = A("ps%d" % bank, 0, 128)
+    def mm(bank, w, x, start=True, stop=True, n=128):
+        o = A("ps%d" % bank, 0, n)
         run("P", lambda: g.tensor.matmul_mx(o[0], w[0][0], w[1][0], x[0][0], x[1][0], start, stop),
             [o], [w[0], w[1], x[0], x[1]], chain=not start)
 
-    def send(t, m):
+    def send(name, to, frm, pairs):
+        rid, pid, _se = topo.addr(to)
+        arr, left = "arr" + name, "left" + name
+        src, land = regs([s for (d, s) in pairs]), regs([d for (d, s) in pairs])
+        before("G", [], src)
+        for (d, s) in pairs:
+            g.remote_dma(d[0], s[0], T.sem[arr], T.sem[left], pid, rid, topo.mask(core, to))
+        total[arr], total[left] = len(pairs) * len(topo.engines(frm, core)), len(pairs) * len(topo.engines(core, to))
+        after((left, total[left], dict(clock["G"])), [], src)
+        after((arr, total[arr], {}), land, [])
+
+    def send_codes(t, m):
         land = M("l%d" % t)
-        before("G", [], m[0][1] + m[1][1])
-        arr, left = "arr%d" % t, "left%d" % t
-        g.remote_dma(by(land[0])[0], by(m[0])[0], T.sem[arr], T.sem[left], pid, rid, mask)
-        g.remote_dma(land[1][0], m[1][0], T.sem[arr], T.sem[left], pid, rid, mask)
-        total[arr], total[left] = 2 * n_in, 2 * n_eng
-        after((left, 2 * n_eng, dict(clock["G"])), [], m[0][1] + m[1][1])
-        after((arr, 2 * n_in, {}), land[0][1] + land[1][1], [])
+        send("c%d" % t, nxt, prv, [(by(land[0]), by(m[0])), (land[1], m[1])])
+
+    def send_back(t):
+        send("b%d" % t, prv, nxt, [(A("lb", 24 * t, 24 * t + 24), A("ub", 24 * t, 24 * t + 24))])
 
     def PS(b, n=128):
         return A("ps%d" % b, 0, n)
@@ -189,40 +194,39 @@ def rank_program(g, core, T, topo):
     def col(name, i):
         return A(name, i, i + 1)
 
-    dma("Y", "x0", A("x0"), T.x[:, 0:512])
-    dma("S", "u", A("ut"), T.u[:])
-    dma("Y", "x1", A("x1"), T.x[:, 512:1024])
+    dma("Y", "x0", A("xx", 0, 512), T.x[:, 0:512])
+    dma("S", "x1", A("xx", 512, 1024), T.x[:, 512:1024])
+    dma("Y", "u", A("ut"), T.u[:])
     dma("Y", "hc", A("hci", 0, 3), T.hc[:])
     dma("Y", "wc", by(A("qww")), T.wc[:])
     dma("Y", "ws", A("sww"), T.ws[:])
     dma("Y", "v", A("vt"), T.v[:])
 
+    iota(A("t4"), [[0, 16], [1, 4]], 0)
     iota(A("pi", 0, 1), [[0, 1]], 0, 1)
-    iota(A("ids"), [[1, 128]], 0)
-    iota(A("t4"), [[0, 8], [1, 4]], 0)
-    iota(A("t16"), [[0, 8], [1, 16]], 0)
     iota(A("gm"), [[1, 8], [0, 16]], 0)
+    iota(A("ids"), [[1, 128]], 0)
+    iota(A("t16"), [[0, 8], [1, 16]], 0)
     iota(A("c16"), [[16, 8]], 0)
     iota(A("pk", 0, 6), [[4, 3], [0, 2]], 0)
+    for s in range(3):
+        iota(third("nhb", s), [[0, 8]], 383 - 64 * SLOT[s])
     pfl, jf, gf, af, bf_, kf = [col("pf32", i) for i in range(6)]
-    fill(A("sgt"), 0.0)
+    act(A("mul"), A("t4", 0, 16), Act.Exp, None, -8 * LN2)
+    fill(A("kbt"), 0.0)
+    fill(A("xs"), 0.0)
+    fill(A("sd"), 0.0)
     ts(col("pi", 1), col("pi", 0), 15, Op.bitwise_and)
     ts(col("pi", 2), col("pi", 0), 4, Op.arith_shift_right)
     ts(col("pi", 3), col("pi", 0), 2, Op.arith_shift_right, 3, Op.bitwise_and)
     ts(col("pi", 4), col("pi", 0), 3, Op.bitwise_and)
-    fill(A("xs"), 0.0)
-    fill(A("sd"), 0.0)
+    fill(A("he", 0, 32, 2), 0.0)
+    fill(A("sv", 0, 40, 5), 0.0)
+    fill(A("sv", 4, 40, 5), 1024.0)
     cp(A("pf32", 0, 5), A("pi", 0, 5))
     act(col("pw", 0), jf, Act.Exp, None, LN2)
     act(col("pw", 1), jf, Act.Exp, 15 * LN2, -LN2)
     act(A("pf32", 6, 8), A("pw", 0, 2))
-    fill(A("kbt"), 0.0)
-    ts(A("eye"), A("ids"), pfl, Op.is_equal)
-    for b in range(4):
-        for t in range(4):
-            act(A("et", 512 * b + t, 512 * b + 512, 4), A("eye"), Act.Copy, None, float(t == b))
-    for b in range(4):
-        act(A("et6", 512 * b, 512 * b + 512), A("et", 512 * b, 512 * b + 512), Act.Copy, None, 64.0)
 
     def selector(out, pos, c, big, period, n, tmp):
         def first():
@@ -231,117 +235,100 @@ def rank_program(g, core, T, topo):
         return [first, lambda: tt(A(out, 0, n), A(tmp, 0, n), A(tmp, n, 2 * n), Op.add),
                 lambda: ts(A(out, period - 1, n, period), A(out, period - 1, n, period), -2.0 * big, Op.add)]
 
-    s4 = selector("sel4", "t4", af, 65536.0, 4, 32, "dx")
+    s4 = selector("sel4", "t4", af, 65536.0, 4, 64, "dx")
     s16 = selector("sel", "t16", jf, 256.0, 16, 128, "cx")
     s4[0]()
-    fill(A("he", 0, 32, 2), 0.0)
-    fill(A("sv", 0, 40, 5), 0.0)
-    fill(A("sv", 4, 40, 5), 1024.0)
+    fill(A("sgt", 256, 512), 0.0)
     s4[1]()
-    for f in range(4):
-        ts(A("tab", 16 * f, 16 * f + 16), A("t16", 0, 16), jf, Op.is_equal, (1.0, 256.0, 65536.0, -2.0 ** -40)[f], Op.mult)
+    ts(A("eye"), A("ids"), pfl, Op.is_equal)
+    ts(kf, af, 2.0, Op.min)
+    ts(col("pf32", 8), bf_, 3.0, Op.is_equal, 4.0, Op.mult)
     s4[2]()
-    quant(M("a0"), A("x0"))
-    send(0, M("a0"))
-    for s in range(3):
-        iota(third("nhb", s), [[0, 8]], 383 - 64 * SLOT[s])
+    for b in range(4):
+        for t in range(4):
+            act(A("et", 512 * b + t, 512 * b + 512, 4), A("eye"), Act.Copy, None, float(t == b))
+    quant(M("aa"), A("xx"))
+    quant(M("uu"), A("ut"))
+    send_codes(0, M("aa", 0, 128))
     iota(A("flt"), [[0, 512]], 0)
     for name, n in (("gw", 3), ("tw", 4), ("mw", 4), ("ew", 4)):
         for b in range(n):
             iota(A(name, 144 * b + 128, 144 * b + 144), [[0, 16]], 0)
-    quant(M("uu"), A("ut"))
-    quant(M("a1"), A("x1"))
-    for i in range(2):
-        ts(plane("bk", i), A("gm"), gf, Op.is_equal, col("pf32", 6 + i), Op.mult)
-    cp(A("hcf", 0, 3), A("hci", 0, 3))
-    ts(A("iw"), A("c16"), jf, Op.add)
-    for t in range(4):
-        cp(A("kbt", 5 * t, 512, 16), A("bk", t, 128, 4))
-    cp(A("kbt", 512, 1024, 4), plane("bk", 1))
-    ts(kf, af, 2.0, Op.min)
-    ts(col("pf32", 8), bf_, 3.0, Op.is_equal, 4.0, Op.mult)
-    quant(M("kb"), A("kbt"))
     KW, BW = M("kb", 0, 128), M("kb", 128, 256)
+    E = [M("ee", 128 * b, 128 * b + 128) for b in range(4)]
+    E6 = [M("e6", 128 * b, 128 * b + 128) for b in range(4)]
 
     def nothing():
         return None
 
-    def addresses(q, a=nothing, b=nothing, c=nothing, d=nothing):
-        mm(4, M("uu"), q)
-        ts(A("sgt", 0, 128), PS(4), 0.0, Op.is_gt)
+    def addresses(q, halves, z=nothing, a=nothing, b=nothing, c=nothing, d=nothing):
+        n = 128 * halves
+        mm(4, M("uu"), q, True, True, n)
+        z()
+        ts(A("sgt", 0, n), PS(4, n), 0.0, Op.is_gt)
         a()
         quant(M("sg"), A("sgt"))
         mm(5, KW, M("sg"))
         b()
-        scan(A("ks"), PS(5, 32), A("sel4"), -65536.0, Op.max, Op.add)
+        scan(A("ks", 0, n // 4), PS(5, n // 4), A("sel4", 0, n // 4), -65536.0, Op.max, Op.add)
         c()
-        for s in range(3):
-            ts(third("pr", s), A("ks", 3, 32, 4), 65536.0, Op.add, col("hcf", SLOT[s]), Op.mult)
+        for h in range(halves):
+            for s in range(3):
+                ts(third("pr", 3 * h + s), A("ks", 32 * h + 3, 32 * h + 32, 4), 65536.0, Op.add, col("hcf", SLOT[s]), Op.mult)
         d()
-        ts(A("hh"), A("pr"), 8, Op.arith_shift_right, 63, Op.bitwise_and)
+        ts(A("hh", 0, 24 * halves), A("pr", 0, 24 * halves), 8, Op.arith_shift_right, 63, Op.bitwise_and)
 
-    def lists_a():
-        ts(col("upk", 0), col("pf32", 8), kf, Op.add)
-        ts(A("urep"), A("pk", 0, 6), bf_, Op.add)
+    def key_tiles():
+        for i in range(2):
+            ts(plane("bk", i), A("gm"), gf, Op.is_equal, col("pf32", 6 + i), Op.mult)
+        cp(A("hcf", 0, 3), A("hci", 0, 3))
+        ts(A("iw"), A("c16"), jf, Op.add)
+        for t in range(4):
+            cp(A("kbt", 5 * t, 512, 16), A("bk", t, 128, 4))
+        cp(A("kbt", 512, 1024, 4), plane("bk", 1))
 
     def lists_b():
+        ts(col("upk", 0), col("pf32", 8), kf, Op.add)
+        ts(A("urep"), A("pk", 0, 6), bf_, Op.add)
+        fill(A("mul", 3, 16, 4), 1.0)
         for f in range(4):
-            fill(A("mul", f, 16, 4), (1.0, 2.0 ** -8, 2.0 ** -16, 1.0)[f])
-        s16[0]()
+            ts(A("tab", 16 * f, 16 * f + 16), A("t16", 0, 16), jf, Op.is_equal, (1.0, 256.0, 65536.0, -2.0 ** -40)[f], Op.mult)
+
+    def clear():
+        fill(A("ow"), 128.0)
+        cp(A("sd", 4, 40, 5), A("iw"))
 
     def outputs(h, qa, qb):
         q = M("fin", 128 * h, 128 * h + 128)
-        mm(6, M("vv"), q)
+        mm(7, M("vv"), q)
         dma(qa, "oc%d" % h, T.oc[:, 512 * h:512 * h + 512], by(q[0]))
         for i in range(4):
             dma((qb, qa)[i % 2], "s%s%d" % ("abcd"[i], h), T.osc[4 * i:4 * i + 4, 128 * h:128 * h + 128],
                 (T.sfin[32 * i:32 * i + 4, 128 * h:128 * h + 128], q[1][1]))
-        cp(plane("yo", h), PS(6))
+        cp(plane("yo", h), PS(7))
         dma(qb, "y%d" % h, T.y[:, 128 * h:128 * h + 128], plane("yo", h))
 
-    E = [M("ee", 128 * b, 128 * b + 128) for b in range(4)]
-    E6 = [M("e6", 128 * b, 128 * b + 128) for b in range(4)]
-    readers = [M("a1"), M("a0"), M("b1")]
+    writers = [M("aa"), M("b1"), M("fin", 0, 128)]
+    readers = [M("aa", 128, 256), M("aa", 0, 128), M("b1")]
     made = [M("b1"), M("fin", 0, 128), M("fin", 128, 256)]
     S6 = 0.015625
     ROUND = 1.5 * 2.0 ** 50
 
     for t in range(3):
-        def clear():
-            fill(A("ow"), 128.0)
-            cp(A("sd", 4, 40, 5), A("iw"))
-
-        if t == 0:
-            addresses(readers[t], lists_a, lists_b, s16[1], clear)
-            s16[2]()
-        else:
-            addresses(readers[t], nothing, clear)
-        tt(A("rn"), A("nhb"), A("hh"), Op.subtract)
-        if t == 0:
-            quant(M("ee"), A("et"))
-        if t == 1:
-            quant(M("vv"), A("vt"))
-        cp(A("urn"), A("rn"))
-        if t == 0:
-            cp(plane("sel", 1), plane("sel", 0))
-            cp(plane("sel", 2), plane("sel", 0))
-        if t == 2:
-            outputs(0, "Y", "Y")
         land = M("l%d" % t)
 
-        def scaled(b):
+        def unit(b):
             if t == 0:
-                quant(E6[b], A("et6", 512 * b, 512 * b + 512))
+                quant(E[b], A("et", 512 * b, 512 * b + 512))
 
-        def unpack():
-            for b in range(4):
-                mm(b, E[b], land)
-            scaled(0)
-
-        addresses(land, nothing, unpack)
-        cp(A("uh"), A("hh"))
-        ts(A("hb"), A("hh"), 1.0625, Op.mult, 159.53, Op.add)
-        tt(A("nh"), A("nhb"), A("hh"), Op.subtract)
+        if t == 0:
+            addresses(writers[t], 2, key_tiles, lambda: quant(M("kb"), A("kbt")), lists_b, s16[0],
+                      lambda: cp(A("sd", 4, 40, 5), A("iw")))
+        else:
+            addresses(writers[t], 1)
+        cp(A("uh"), A("hh", 0, 24))
+        ts(A("hb"), A("hh", 0, 24), 1.0625, Op.mult, 159.53, Op.add)
+        tt(A("nh", 0, 24), A("nhb"), A("hh", 0, 24), Op.subtract)
         ends = A("cur", 4, 40, 5)
 
         for p in range(3):
@@ -365,26 +352,51 @@ def rank_program(g, core, T, topo):
                 for f in range(3):
                     act(A("m96", f, 96, 4), A("sn", 24 * f, 24 * f + 24), Act.Relu, None, 2.0 ** 17)
                 act(A("m96", 3, 96, 4), A("pp"), Act.Copy, None, -2048.0 * (1.0 + 2.0 ** -18))
-                for b in range(4):
-                    act(window("tw", b, 128), PS(b))
-                act(plane("za", 0), PS(0))
             else:
                 for s in range(3):
                     tt(A("m96", 32 * s + 3, 32 * s + 32, 4), A("m96", 32 * s + 3, 32 * s + 32, 4), A("lf"), Op.mult)
+            if p == 2:
+                for b in range(4):
+                    act(window("tw", b, 128), PS(b))
+                act(plane("za", 0), PS(0))
+            if t == 0 and p < 2:
+                for b in (2 * p, 2 * p + 1):
+                    act(A("et6", 512 * b, 512 * b + 512), A("et", 512 * b, 512 * b + 512), Act.Copy, None, 64.0)
             ts(A("gy"), dst[0], 0.0, Op.is_lt)
             total_of(col("xs", 0), dst[0])
             total_of(col("xs", 4), A("gy"))
             tt(A("n1"), IND(A("xs"), col("upk", 0)), A("mul"), Op.mult)
+            if p == 0 and t == 0:
+                tt(A("nh", 24, 48), A("nhb"), A("hh", 24, 48), Op.subtract)
             ts(A("n2"), A("n1"), 255, Op.bitwise_and)
+            if p == 0 and t == 0:
+                cp(A("ub", 0, 24), A("nh", 24, 48))
+                send_back(0)
+            if p == 0 and t < 2:
+                cp(A("ub", 24 * t + 24, 24 * t + 48), A("nh", 0, 24))
+                send_back(t + 1)
             ts(A("flt", 0, 384, 4), IND(A("n2"), A("urep")), 1.0, Op.is_equal, col("hb", 0), Op.min)
+            if p < 2:
+                unit(2 * p)
             quant(M("fl"), A("flt"))
             mm(6, BW, M("fl"))
+            if p < 2:
+                unit(2 * p + 1)
+            if p == 0 and t == 0:
+                s16[1]()
             if p == 1:
+                for b in range(4):
+                    mm(b, E[b], land)
                 tt(A("hv", 0, 16, 2), third("nh", 2), third("nh", 0), Op.subtract)
                 tt(A("hv", 16, 32, 2), third("nh", 2), third("nh", 1), Op.subtract)
                 cp(A("hv", 1, 32, 2), A("nh", 0, 16))
-            scaled(p + 1)
+            if p == 2 and t == 0:
+                fill(A("ow"), 128.0)
+                cp(plane("sel", 1), plane("sel", 0))
+                cp(plane("sel", 2), plane("sel", 0))
             scan(A("y1"), PS(6, 96), A("m96"), 0.0, Op.max, Op.mult)
+            if p == 0 and t == 0:
+                s16[2]()
             ts(A("yr"), A("y1", 3, 96, 4), ROUND, Op.add, ROUND, Op.subtract)
             for s in range(3):
                 tt(A("sd", PLACE[s], 40, 5), A("y1", 32 * s + 3, 32 * s + 32, 4), third("yr", s), Op.subtract)
@@ -402,14 +414,27 @@ def rank_program(g, core, T, topo):
         cp(A("uhab"), A("hab", 1, 32, 2))
         act(plane("og", 1), IND(A("ow"), A("uhab", 8, 16)))
         cp(plane("og", 0), IND(A("ow"), A("uhab", 0, 8)))
-        act(plane("rg", 0), IND(A("ow"), A("urn", 0, 8)))
+        for s in range(3):
+            act(plane("rg", s), IND(A("ow"), third("lb", 3 * t + s)))
         scan(A("osn"), A("og"), A("sel", 0, 256), -256.0, Op.max, Op.add)
         ts(A("uo"), A("osn", 15, 256, 16), 256.0, Op.add)
-        oa, ob = A("uo", 0, 8), A("uo", 8, 16)
+        send("o%d" % t, nxt, prv, [(A("lo", 16 * t, 16 * t + 16), A("uo"))])
+        if t == 0:
+            for b in range(4):
+                quant(E6[b], A("et6", 512 * b, 512 * b + 512))
+        scan(A("rsn"), A("rg"), A("sel"), -256.0, Op.max, Op.add)
+        if t == 0:
+            quant(M("vv"), A("vt"))
+        ts(A("urd"), A("rsn", 15, 384, 16), 256.0, Op.add)
+        send("r%d" % t, nxt, prv, [(A("lr", 24 * t, 24 * t + 24), A("urd"))])
+        if t < 2:
+            clear()
+        else:
+            outputs(0, "Y", "Y")
+        oa, ob = third("lo", 2 * t), third("lo", 2 * t + 1)
 
         for b in range(1, 4):
             act(plane("za", b), IND(window("tw", b), oa))
-        act(plane("rg", 1), IND(A("ow"), A("urn", 8, 16)))
         tt(plane("tt", 0), IND(window("tw", 0), oa), plane("za", 0), Op.subtract)
         tt(plane("tt", 1), PS(1), plane("za", 1), Op.subtract)
         tt(window("mw", 0, 128), IND(window("tw", 0), ob), plane("tt", 0), Op.add)
@@ -421,7 +446,6 @@ def rank_program(g, core, T, topo):
                 tt(plane("tt", 0), PS(0), plane("za", 0), Op.add)
             tt(window("mw", b, 128), IND(window("tw", b), ob), plane("tt", b), Op.subtract)
             act(plane("za", b), IND(window("mw", b), oa))
-        act(plane("rg", 2), IND(A("ow"), A("urn", 16, 24)))
         for b in range(4):
             if b < 3:
                 tt(plane("tt", b + 1), PS(b + 1), plane("za", b + 1), Op.add)
@@ -431,21 +455,19 @@ def rank_program(g, core, T, topo):
             mm(4 + b, E[b], M("nn"))
         for b in range(4):
             mm(b, E6[b], readers[t], True, False)
-        scan(A("rsn"), A("rg"), A("sel"), -256.0, Op.max, Op.add)
-        ts(A("urd"), A("rsn", 15, 384, 16), 256.0, Op.add)
 
+        rd = [third("lr", 3 * t + s) for s in range(3)]
         act(window("ew", 0, 128), PS(4))
         cp(window("ew", 1, 128), PS(5))
         cp(window("ew", 2, 128), PS(6))
+        cp(window("ew", 3, 128), PS(7))
         for b in range(4):
-            if b == 2:
-                act(window("ew", 3, 128), PS(7))
-            act(plane("za", b), IND(window("ew", b), A("urd", 0, 8)))
+            act(plane("za", b), IND(window("ew", b), rd[0]))
         for b in range(5):
             if b < 4:
-                tt(plane("tt", b), IND(window("ew", b), A("urd", 16, 24)), plane("za", b), Op.add)
+                tt(plane("tt", b), IND(window("ew", b), rd[2]), plane("za", b), Op.add)
             if b > 0:
-                tt(A("ft", b - 1, 512, 4), IND(window("ew", b - 1), A("urd", 8, 16)), plane("tt", b - 1), Op.add)
+                tt(A("ft", b - 1, 512, 4), IND(window("ew", b - 1), rd[1]), plane("tt", b - 1), Op.add)
         quant(M("ff"), A("ft"))
         for b in (0, 2, 1, 3):
             mm(b, M("ww", 128 * b, 128 * b + 128), M("ff"), False, True)
@@ -454,7 +476,7 @@ def rank_program(g, core, T, topo):
             act(A("xn", b + 2, 512, 4), PS(b + 2), Act.Copy, None, S6)
         quant(made[t], A("xn"))
         if t < 2:
-            send(t + 1, made[t])
+            send_codes(t + 1, made[t])
 
     outputs(1, "Y", "S")
     for sem, val in total.items():

import math
from concourse.mybir import dt, AluOpType as Op, ActivationFunctionType as Act, AxisListType

X4, U8, BF, F32, I32, U16 = "float8_e4m3fn_x4", "uint8", "bfloat16", "float32", "int32", "uint16"
SCRATCH = {}
for _n, _w in dict(aa=256, b1=128, fin=256, l0=128, l1=128, l2=128, uu=128, vv=128, ww=512, ee=512, e6=512,
                   kb=256, sg=128, fl=128, nn=128, ff=128).items():
    SCRATCH["q" + _n] = ("sbuf", [128, _w], X4)
    SCRATCH["s" + _n] = ("sbuf", [128, _w], U8)
for _k, _d in (
        (BF, dict(xx=1024, ut=512, vt=512, et=2048, et6=2048, kbt=1024, sgt=512, flt=512, nt=512, ft=512,
                  xn=512, ids=128, gm=128, t16=128, bk=256, pw=4, tab=64, gw=432, gx=384, ow=384, tw=576,
                  mw=576, ew=576, za=512, og=256, rg=384, sel=384, cx=256, eye=128, hb=24, sn=72, pp=24,
                  osn=256, rsn=384, gy=128, gj=256, mul=16)),
        (F32, dict(pf32=10, t4=64, sel4=64, dx=128, hcf=4, ks=64, xs=8, y1=96, tt=512, yo=256, m96=96,
                   yr=24, sd=40, sv=40, cur=40, lf=8, he=32, hv=32, hab=32)),
        (I32, dict(pi=8, c16=8, iw=8, pk=8, nhb=24, hci=4, pr=48, hh=48, nh=48, n1=16, n2=16)),
        (U16, dict(upk=2, urep=6, uh=24, ub=72, lb=72, uidx=8, uown=8, uhab=16, uo=16, urd=24, lo=48, lr=72))):
    for _n, _w in _d.items():
        SCRATCH[_n] = ("sbuf", [128, _w], _k)
for _n in range(8):
    SCRATCH["ps%d" % _n] = ("psum", [128, 512], F32)

_DMAS = ["x0", "x1", "u", "v", "hc", "wc", "ws"] + ["%s%d" % (_n, _h) for _h in range(2) for _n in ("y", "oc", "sa", "sb", "sc", "sd")]
SEMAPHORES = (["V", "S", "P", "G"] + ["d_" + _n for _n in _DMAS]
              + ["%s%s%d" % (_a, _n, _t) for _a in ("arr", "left") for _n in "cbor" for _t in range(3)])

SLOT = (0, 2, 1)
PLACE = (3, 1, 2)
LN2 = math.log(2.0)


def rank_program(g, core, T, topo):
    rank = T.rank_of(core)
    if rank is None:
        return
    nxt, prv = T.cores[(rank + 1) % len(T.cores)], T.cores[rank - 1]

    eng = {"V": g.vector, "S": g.scalar, "P": g.tensor, "G": g, "Y": g.sync}
    total = {}
    clock = {q: {} for q in eng}
    hist = {}

    def A(name, lo=0, hi=None, step=1):
        if hi is None:
            hi = SCRATCH[name][1][1]
        ap = T[name][:, lo:hi] if step == 1 else T[name][:, lo:hi:step]
        return (ap, [(name, lo, hi, step)])

    def IND(win, off):
        return (win[0].indirect(off[0]), win[1] + off[1])

    def meets(a, b):
        if a[0].startswith("ps"):
            return True
        if a[2] <= b[1] or b[2] <= a[1]:
            return False
        return not (a[3] == b[3] and a[3] > 1 and (a[1] - b[1]) % a[3] != 0)

    def wait(q, ev):
        sem, val, snap = ev
        if clock[q].get(sem, 0) >= val:
            return
        eng[q].wait_ge(T.sem[sem], val)
        for k, x in snap.items():
            if clock[q].get(k, 0) < x:
                clock[q][k] = x
        clock[q][sem] = val

    def before(q, writes, reads, chain=False):
        need = []
        for regs, w in ((writes, True), (reads, False)):
            for r in regs:
                for (o, ow, ev) in hist.get(r[0], []):
                    if (w or ow or r[0].startswith("ps")) and meets(r, o):
                        if chain and r[0].startswith("ps") and ev[0] == "P":
                            continue
                        need.append(ev)
        need.sort(key=lambda e: -e[1])
        for ev in need:
            wait(q, ev)

    def after(ev, writes, reads):
        for r in writes:
            hist.setdefault(r[0], []).append((r, True, ev))
        for r in reads:
            hist.setdefault(r[0], []).append((r, False, ev))

    def regs(xs):
        return [r for x in xs if isinstance(x, tuple) for r in x[1]]

    def ap(x):
        return x[0] if isinstance(x, tuple) else x

    def run(q, make, outs, ins, chain=False):
        w, r = regs(outs), regs(ins)
        before(q, w, r, chain)
        total[q] = total.get(q, 0) + 1
        make().then_inc(T.sem[q], 1)
        after((q, total[q], dict(clock[q])), w, r)

    def dma(q, name, out, in_):
        w, r = regs([out]), regs([in_])
        before(q, w, r)
        sem = "d_" + name
        total[sem] = 16
        eng[q].dma_start(ap(out), ap(in_)).then_inc(T.sem[sem], 16)
        after((sem, 16, dict(clock[q])), w, r)

    def by(x):
        return (x[0].bitcast(dt.uint8), x[1])

    V = g.vector

    def cp(o, i, scatter=None):
        if scatter is None:
            run("V", lambda: V.tensor_copy(o[0], i[0]), [o], [i])
        else:
            run("V", lambda: V.tensor_copy(o[0].indirect(scatter[0]), i[0]), [o], [i, scatter])

    def tt(o, a, b, op):
        run("V", lambda: V.tensor_tensor(o[0], a[0], b[0], op), [o], [a, b])

    def ts(o, a, s1, op0, s2=None, op1=None):
        if op1 is None:
            run("V", lambda: V.tensor_scalar(o[0], a[0], ap(s1), None, op0), [o], [a, s1])
        else:
            run("V", lambda: V.tensor_scalar(o[0], a[0], ap(s1), ap(s2), op0, op1), [o], [a, s1, s2])

    def scan(o, a, b, init, op0, op1):
        run("V", lambda: V.tensor_tensor_scan(o[0], a[0], b[0], init, op0, op1), [o], [a, b])

    def total_of(o, i):
        run("V", lambda: V.tensor_reduce(o[0], i[0], AxisListType.X, Op.add), [o], [i])

    def fill(o, c):
        run("V", lambda: V.memset(o[0], c), [o], [])

    def act(o, i, func=Act.Copy, bias=None, scale=1.0, acc=None):
        if acc is not None:
            run("S", lambda: g.scalar.activation(o[0], i[0], func, scale=scale, accum_out=acc[0]), [o, acc], [i])
        elif bias is None:
            run("S", lambda: g.scalar.activation(o[0], i[0], func, scale=scale), [o], [i])
        else:
            run("S", lambda: g.scalar.activation(o[0], i[0], func, bias=bias, scale=scale), [o], [i])

    def iota(o, pattern, base, mult=0):
        if SCRATCH[o[1][0][0]][2] == I32:
            run("G", lambda: g.iota(o[0], pattern, base, mult), [o], [])
        else:
            run("G", lambda: g.iota(o[0], pattern, base, mult, allow_small_or_imprecise_dtypes=True), [o], [])

    def M(name, lo=0, hi=None):
        return (A("q" + name, lo, hi), A("s" + name, lo, hi))

    def quant(m, t):
        run("V", lambda: V.quantize_mx(m[0][0], m[1][0], t[0]), [m[0], m[1]], [t])

    def mm(bank, w, x, start=True, stop=True, n=128):
        o = A("ps%d" % bank, 0, n)
        run("P", lambda: g.tensor.matmul_mx(o[0], w[0][0], w[1][0], x[0][0], x[1][0], start, stop),
            [o], [w[0], w[1], x[0], x[1]], chain=not start)

    def send(name, to, frm, pairs):
        rid, pid, _se = topo.addr(to)
        arr, left = "arr" + name, "left" + name
        src, land = regs([s for (d, s) in pairs]), regs([d for (d, s) in pairs])
        before("G", [], src)
        for (d, s) in pairs:
            g.remote_dma(d[0], s[0], T.sem[arr], T.sem[left], pid, rid, topo.mask(core, to))
        total[arr], total[left] = len(pairs) * len(topo.engines(frm, core)), len(pairs) * len(topo.engines(core, to))
        after((left, total[left], dict(clock["G"])), [], src)
        after((arr, total[arr], {}), land, [])

    def send_codes(t, m):
        land = M("l%d" % t)
        send("c%d" % t, nxt, prv, [(by(land[0]), by(m[0])), (land[1], m[1])])

    def send_back(t):
        send("b%d" % t, prv, nxt, [(A("lb", 24 * t, 24 * t + 24), A("ub", 24 * t, 24 * t + 24))])

    def PS(b, n=128):
        return A("ps%d" % b, 0, n)

    def plane(name, b):
        return A(name, 128 * b, 128 * b + 128)

    def window(name, b, n=144):
        return A(name, 144 * b, 144 * b + n)

    def third(name, s):
        return A(name, 8 * s, 8 * s + 8)

    def col(name, i):
        return A(name, i, i + 1)

    dma("Y", "x0", A("xx", 0, 512), T.x[:, 0:512])
    dma("S", "x1", A("xx", 512, 1024), T.x[:, 512:1024])
    dma("Y", "u", A("ut"), T.u[:])
    dma("Y", "hc", A("hci", 0, 3), T.hc[:])
    dma("Y", "wc", by(A("qww")), T.wc[:])
    dma("Y", "ws", A("sww"), T.ws[:])
    dma("Y", "v", A("vt"), T.v[:])

    iota(A("t4"), [[0, 16], [1, 4]], 0)
    iota(A("pi", 0, 1), [[0, 1]], 0, 1)
    iota(A("gm"), [[1, 8], [0, 16]], 0)
    iota(A("ids"), [[1, 128]], 0)
    iota(A("t16"), [[0, 8], [1, 16]], 0)
    iota(A("c16"), [[16, 8]], 0)
    iota(A("pk", 0, 6), [[4, 3], [0, 2]], 0)
    for s in range(3):
        iota(third("nhb", s), [[0, 8]], 383 - 64 * SLOT[s])
    pfl, jf, gf, af, bf_, kf = [col("pf32", i) for i in range(6)]
    act(A("mul"), A("t4", 0, 16), Act.Exp, None, -8 * LN2)
    fill(A("kbt"), 0.0)
    fill(A("xs"), 0.0)
    fill(A("sd"), 0.0)
    ts(col("pi", 1), col("pi", 0), 15, Op.bitwise_and)
    ts(col("pi", 2), col("pi", 0), 4, Op.arith_shift_right)
    ts(col("pi", 3), col("pi", 0), 2, Op.arith_shift_right, 3, Op.bitwise_and)
    ts(col("pi", 4), col("pi", 0), 3, Op.bitwise_and)
    fill(A("he", 0, 32, 2), 0.0)
    fill(A("sv", 0, 40, 5), 0.0)
    fill(A("sv", 4, 40, 5), 1024.0)
    cp(A("pf32", 0, 5), A("pi", 0, 5))
    act(col("pw", 0), jf, Act.Exp, None, LN2)
    act(col("pw", 1), jf, Act.Exp, 15 * LN2, -LN2)
    act(A("pf32", 6, 8), A("pw", 0, 2))

    def selector(out, pos, c, big, period, n, tmp):
        def first():
            ts(A(tmp, 0, n), A(pos, 0, n), c, Op.is_equal, big, Op.mult)
            ts(A(tmp, n, 2 * n), A(pos, 0, n), c, Op.is_lt, -2.0 * big, Op.mult)
        return [first, lambda: tt(A(out, 0, n), A(tmp, 0, n), A(tmp, n, 2 * n), Op.add),
                lambda: ts(A(out, period - 1, n, period), A(out, period - 1, n, period), -2.0 * big, Op.add)]

    s4 = selector("sel4", "t4", af, 65536.0, 4, 64, "dx")
    s16 = selector("sel", "t16", jf, 256.0, 16, 128, "cx")
    s4[0]()
    fill(A("sgt", 256, 512), 0.0)
    s4[1]()
    ts(A("eye"), A("ids"), pfl, Op.is_equal)
    ts(kf, af, 2.0, Op.min)
    ts(col("pf32", 8), bf_, 3.0, Op.is_equal, 4.0, Op.mult)
    s4[2]()
    for b in range(4):
        for t in range(4):
            act(A("et", 512 * b + t, 512 * b + 512, 4), A("eye"), Act.Copy, None, float(t == b))
    quant(M("aa"), A("xx"))
    quant(M("uu"), A("ut"))
    send_codes(0, M("aa", 0, 128))
    iota(A("flt"), [[0, 512]], 0)
    for name, n in (("gw", 3), ("tw", 4), ("mw", 4), ("ew", 4)):
        for b in range(n):
            iota(A(name, 144 * b + 128, 144 * b + 144), [[0, 16]], 0)
    KW, BW = M("kb", 0, 128), M("kb", 128, 256)
    E = [M("ee", 128 * b, 128 * b + 128) for b in range(4)]
    E6 = [M("e6", 128 * b, 128 * b + 128) for b in range(4)]

    def nothing():
        return None

    def addresses(q, halves, z=nothing, a=nothing, b=nothing, c=nothing, d=nothing):
        n = 128 * halves
        mm(4, M("uu"), q, True, True, n)
        z()
        ts(A("sgt", 0, n), PS(4, n), 0.0, Op.is_gt)
        a()
        quant(M("sg"), A("sgt"))
        mm(5, KW, M("sg"))
        b()
        scan(A("ks", 0, n // 4), PS(5, n // 4), A("sel4", 0, n // 4), -65536.0, Op.max, Op.add)
        c()
        for h in range(halves):
            for s in range(3):
                ts(third("pr", 3 * h + s), A("ks", 32 * h + 3, 32 * h + 32, 4), 65536.0, Op.add, col("hcf", SLOT[s]), Op.mult)
        d()
        ts(A("hh", 0, 24 * halves), A("pr", 0, 24 * halves), 8, Op.arith_shift_right, 63, Op.bitwise_and)

    def key_tiles():
        for i in range(2):
            ts(plane("bk", i), A("gm"), gf, Op.is_equal, col("pf32", 6 + i), Op.mult)
        cp(A("hcf", 0, 3), A("hci", 0, 3))
        ts(A("iw"), A("c16"), jf, Op.add)
        for t in range(4):
            cp(A("kbt", 5 * t, 512, 16), A("bk", t, 128, 4))
        cp(A("kbt", 512, 1024, 4), plane("bk", 1))

    def lists_b():
        ts(col("upk", 0), col("pf32", 8), kf, Op.add)
        ts(A("urep"), A("pk", 0, 6), bf_, Op.add)
        fill(A("mul", 3, 16, 4), 1.0)
        for f in range(4):
            ts(A("tab", 16 * f, 16 * f + 16), A("t16", 0, 16), jf, Op.is_equal, (1.0, 256.0, 65536.0, -2.0 ** -40)[f], Op.mult)

    def clear():
        fill(A("ow"), 128.0)
        cp(A("sd", 4, 40, 5), A("iw"))

    def outputs(h, qa, qb):
        q = M("fin", 128 * h, 128 * h + 128)
        mm(7, M("vv"), q)
        dma(qa, "oc%d" % h, T.oc[:, 512 * h:512 * h + 512], by(q[0]))
        for i in range(4):
            dma((qb, qa)[i % 2], "s%s%d" % ("abcd"[i], h), T.osc[4 * i:4 * i + 4, 128 * h:128 * h + 128],
                (T.sfin[32 * i:32 * i + 4, 128 * h:128 * h + 128], q[1][1]))
        cp(plane("yo", h), PS(7))
        dma(qb, "y%d" % h, T.y[:, 128 * h:128 * h + 128], plane("yo", h))

    writers = [M("aa"), M("b1"), M("fin", 0, 128)]
    readers = [M("aa", 128, 256), M("aa", 0, 128), M("b1")]
    made = [M("b1"), M("fin", 0, 128), M("fin", 128, 256)]
    S6 = 0.015625
    ROUND = 1.5 * 2.0 ** 50

    for t in range(3):
        land = M("l%d" % t)

        def unit(b):
            if t == 0:
                quant(E[b], A("et", 512 * b, 512 * b + 512))

        if t == 0:
            addresses(writers[t], 2, key_tiles, lambda: quant(M("kb"), A("kbt")), lists_b, s16[0],
                      lambda: cp(A("sd", 4, 40, 5), A("iw")))
        else:
            addresses(writers[t], 1)
        cp(A("uh"), A("hh", 0, 24))
        ts(A("hb"), A("hh", 0, 24), 1.0625, Op.mult, 159.53, Op.add)
        tt(A("nh", 0, 24), A("nhb"), A("hh", 0, 24), Op.subtract)
        ends = A("cur", 4, 40, 5)

        for p in range(3):
            if p == 0:
                src = [IND(A("tab"), third("uh", s)) for s in range(3)]
                dst = [window("gw", s, 128) for s in range(3)]
            else:
                src = [IND(window("gw", s), A("uidx")) for s in range(3)]
                dst = [plane("gx", s) for s in range(3)]
            for s in (1, 2):
                act(dst[s], src[s], Act.Copy, None, 1.0, col("xs", s))
            for s in (1, 2):
                act(plane("gj", s - 1), dst[s], Act.Relu, None, -2.0 ** 40, col("xs", 4 + s))
            cp(dst[0], src[0])
            if p == 0:
                for s in range(3):
                    cp(A("sv", PLACE[s], 40, 5), third("nh", s))
                for f in range(3):
                    act(A("sn", 24 * f, 24 * f + 24), A("hb"), Act.Sign, 175.5 + 17 * f, -1.0)
                act(A("pp"), A("hb"), Act.Exp, -211 * LN2, LN2)
                for f in range(3):
                    act(A("m96", f, 96, 4), A("sn", 24 * f, 24 * f + 24), Act.Relu, None, 2.0 ** 17)
                act(A("m96", 3, 96, 4), A("pp"), Act.Copy, None, -2048.0 * (1.0 + 2.0 ** -18))
            else:
                for s in range(3):
                    tt(A("m96", 32 * s + 3, 32 * s + 32, 4), A("m96", 32 * s + 3, 32 * s + 32, 4), A("lf"), Op.mult)
            if p == 2:
                for b in range(4):
                    act(window("tw", b, 128), PS(b))
                act(plane("za", 0), PS(0))
            if t == 0 and p < 2:
                for b in (2 * p, 2 * p + 1):
                    act(A("et6", 512 * b, 512 * b + 512), A("et", 512 * b, 512 * b + 512), Act.Copy, None, 64.0)
            ts(A("gy"), dst[0], 0.0, Op.is_lt)
            total_of(col("xs", 0), dst[0])
            total_of(col("xs", 4), A("gy"))
            tt(A("n1"), IND(A("xs"), col("upk", 0)), A("mul"), Op.mult)
            if p == 0 and t == 0:
                tt(A("nh", 24, 48), A("nhb"), A("hh", 24, 48), Op.subtract)
            ts(A("n2"), A("n1"), 255, Op.bitwise_and)
            if p == 0 and t == 0:
                cp(A("ub", 0, 24), A("nh", 24, 48))
                send_back(0)
            if p == 0 and t < 2:
                cp(A("ub", 24 * t + 24, 24 * t + 48), A("nh", 0, 24))
                send_back(t + 1)
            ts(A("flt", 0, 384, 4), IND(A("n2"), A("urep")), 1.0, Op.is_equal, col("hb", 0), Op.min)
            if p < 2:
                unit(2 * p)
            quant(M("fl"), A("flt"))
            mm(6, BW, M("fl"))
            if p < 2:
                unit(2 * p + 1)
            if p == 0 and t == 0:
                s16[1]()
            if p == 1:
                for b in range(4):
                    mm(b, E[b], land)
                tt(A("hv", 0, 16, 2), third("nh", 2), third("nh", 0), Op.subtract)
                tt(A("hv", 16, 32, 2), third("nh", 2), third("nh", 1), Op.subtract)
                cp(A("hv", 1, 32, 2), A("nh", 0, 16))
            if p == 2 and t == 0:
                fill(A("ow"), 128.0)
                cp(plane("sel", 1), plane("sel", 0))
                cp(plane("sel", 2), plane("sel", 0))
            scan(A("y1"), PS(6, 96), A("m96"), 0.0, Op.max, Op.mult)
            if p == 0 and t == 0:
                s16[2]()
            ts(A("yr"), A("y1", 3, 96, 4), ROUND, Op.add, ROUND, Op.subtract)
            for s in range(3):
                tt(A("sd", PLACE[s], 40, 5), A("y1", 32 * s + 3, 32 * s + 32, 4), third("yr", s), Op.subtract)
            scan(A("cur"), A("sd"), A("sv"), 0.0, Op.max, Op.min)
            if p < 2:
                ts(A("uidx"), ends, 128.0, Op.min)
                ts(A("lf"), ends, 128.0, Op.is_lt)
                cp(A("sd", 4, 40, 5), ends)

        ts(A("he", 1, 16, 2), ends, 320.0, Op.is_ge)
        ts(A("he", 17, 32, 2), ends, 256.0, Op.is_lt)
        cp(A("uown"), ends)
        scan(A("hab"), A("he"), A("hv"), 0.0, Op.mult, Op.add)
        cp(A("ow"), A("ids"), A("uown"))
        cp(A("uhab"), A("hab", 1, 32, 2))
        act(plane("og", 1), IND(A("ow"), A("uhab", 8, 16)))
        cp(plane("og", 0), IND(A("ow"), A("uhab", 0, 8)))
        for s in range(3):
            act(plane("rg", s), IND(A("ow"), third("lb", 3 * t + s)))
        scan(A("osn"), A("og"), A("sel", 0, 256), -256.0, Op.max, Op.add)
        ts(A("uo"), A("osn", 15, 256, 16), 256.0, Op.add)
        send("o%d" % t, nxt, prv, [(A("lo", 16 * t, 16 * t + 16), A("uo"))])
        if t == 0:
            for b in range(4):
                quant(E6[b], A("et6", 512 * b, 512 * b + 512))
        scan(A("rsn"), A("rg"), A("sel"), -256.0, Op.max, Op.add)
        if t == 0:
            quant(M("vv"), A("vt"))
        ts(A("urd"), A("rsn", 15, 384, 16), 256.0, Op.add)
        send("r%d" % t, nxt, prv, [(A("lr", 24 * t, 24 * t + 24), A("urd"))])
        if t < 2:
            clear()
        else:
            outputs(0, "Y", "Y")
        oa, ob = third("lo", 2 * t), third("lo", 2 * t + 1)

        for b in range(1, 4):
            act(plane("za", b), IND(window("tw", b), oa))
        tt(plane("tt", 0), IND(window("tw", 0), oa), plane("za", 0), Op.subtract)
        tt(plane("tt", 1), PS(1), plane("za", 1), Op.subtract)
        tt(window("mw", 0, 128), IND(window("tw", 0), ob), plane("tt", 0), Op.add)
        act(plane("za", 0), IND(window("mw", 0), oa))
        for b in range(1, 4):
            if b < 3:
                tt(plane("tt", b + 1), PS(b + 1), plane("za", b + 1), Op.subtract)
            else:
                tt(plane("tt", 0), PS(0), plane("za", 0), Op.add)
            tt(window("mw", b, 128), IND(window("tw", b), ob), plane("tt", b), Op.subtract)
            act(plane("za", b), IND(window("mw", b), oa))
        for b in range(4):
            if b < 3:
                tt(plane("tt", b + 1), PS(b + 1), plane("za", b + 1), Op.add)
            tt(A("nt", b, 512, 4), IND(window("mw", b), ob), plane("tt", b), Op.add)
        quant(M("nn"), A("nt"))
        for b in range(4):
            mm(4 + b, E[b], M("nn"))
        for b in range(4):
            mm(b, E6[b], readers[t], True, False)

        rd = [third("lr", 3 * t + s) for s in range(3)]
        act(window("ew", 0, 128), PS(4))
        cp(window("ew", 1, 128), PS(5))
        cp(window("ew", 2, 128), PS(6))
        cp(window("ew", 3, 128), PS(7))
        for b in range(4):
            act(plane("za", b), IND(window("ew", b), rd[0]))
        for b in range(5):
            if b < 4:
                tt(plane("tt", b), IND(window("ew", b), rd[2]), plane("za", b), Op.add)
            if b > 0:
                tt(A("ft", b - 1, 512, 4), IND(window("ew", b - 1), rd[1]), plane("tt", b - 1), Op.add)
        quant(M("ff"), A("ft"))
        for b in (0, 2, 1, 3):
            mm(b, M("ww", 128 * b, 128 * b + 128), M("ff"), False, True)
        for b in range(2):
            ts(A("xn", b, 512, 4), PS(b), S6, Op.mult)
            act(A("xn", b + 2, 512, 4), PS(b + 2), Act.Copy, None, S6)
        quant(made[t], A("xn"))
        if t < 2:
            send_codes(t + 1, made[t])

    outputs(1, "Y", "S")
    for sem, val in total.items():
        wait("G", (sem, val, {}))
